import numpy as np, ml_dtypes
CORES = [13,21,141,149]
N = 4
BF = ml_dtypes.bfloat16
Y, X, O, S, Q, R = 128, 32, 1024, 2, 512, 3
PL = Y * X
def plain(rng):
    u = 0.5 - 0.5 * np.cos(np.pi * rng.random((N, 8, 16, O)))
    v = np.where((np.arange(8) % 2 == 0)[None, :, None, None], 0.25 + 3.75 * u, (0.5 + 1.5 * u) * np.exp2(rng.integers(-1, 2, (N, 8, 16, 1))))
    return v, rng.integers(0, 16, (N, 8, 16, O)), rng.integers(-7, 8, (N, 3, 128, 128))
def pack(v, z, a):
    a = a.astype(np.float32).astype(BF)
    return {"v0": np.ascontiguousarray(np.clip(v, 0.25, 4.0).reshape(N, 128, O)).astype(np.float32).astype(BF), "z0": np.ascontiguousarray(z.reshape(N, 128, O)).astype(np.float32).astype(BF),
            "ay": np.ascontiguousarray(a[:, 0]), "ax": np.ascontiguousarray(a[:, 1]), "bm": np.ascontiguousarray(a[:, 2])}
def slip():
    s0 = np.arange(208, 256) * 2.0 ** -6; e = np.repeat(s0[None, :], S, axis=0); b = e.copy()
    for t in range(R):
        p = t % S; o = (t - 1) % S
        e[p] = 0.5 * e[p] + 0.25 * np.exp(-np.minimum(0.125 * np.abs(e[p] - e[o]), 0.25)) * e[o]
        c = b.astype(np.float32).astype(BF).astype(np.float64)
        b[p] = 0.5 * b[p] + 0.25 * np.exp(-np.minimum(0.125 * np.abs(c[p] - c[o]), 0.25)) * b[o]
    return s0, np.max(np.abs(e - b), axis=0)
def setup_inputs(rng):
    return pack(*plain(rng))
def setup_inputs_spread(rng):
    v, z, a = plain(rng)
    v = (0.5 + 1.5 * rng.random((N, 8, 16, O))) * np.exp2(rng.integers(-1, 2, (N, 8, 1, O)))
    z = np.minimum((16 * rng.random((N, 8, 16, O)) ** rng.choice(np.array([0.25, 1.0, 4.0]), (N, 8, 16, 1))).astype(np.int64), 15)
    cap = rng.integers(1, 8, (N, 3, 1, 128)); share = rng.choice(np.array([0.2, 0.6, 1.0]), (N, 3, 1, 128))
    a = np.clip(a, -cap, cap) * (rng.random(a.shape) < share)
    return pack(v, z, a)
def setup_inputs_ends(rng):
    base = rng.random((1, 8, 16, 1)) < 0.5
    flip = (rng.random((N, 8, 16, O)) < 1 / 8) ^ (rng.random((N, 8, 1, O)) < 1 / 16)
    flip[:, :, :, 0] = False; flip[:, :, :, O - 1] = True
    v = np.where(base ^ flip, 4.0, 0.25)
    full = np.array([0, O // 2 + 1, O - 2, O - 1]); less = np.array([2, 3, 4, 5, O - 5, O - 4])
    dens = rng.choice(np.array([0, 1 / 32, 1 / 8, 1.0]), (N, 1, 1, O), p=np.array([0.05, 0.55, 0.36, 0.04])); dens[..., full] = 1.0; dens[..., np.array([1, O - 3])] = 0.0; dens[..., less] = 1.0
    z = 15 * (rng.random((N, 8, 16, O)) < dens)
    m = np.where((dens == 1.0) & (rng.random(dens.shape) < 0.5), rng.integers(1, 41, dens.shape), 0); m[..., full] = 0; m[..., less] = 1
    z = np.where(np.argsort(rng.random((N, 128, O)), axis=1).reshape(N, 8, 16, O) < m, 0, z)
    a = rng.choice(np.array([-7, 7]), (N, 3, 128, 128))
    a[:, :2, :, 5::16] = np.where(np.argsort(rng.random((N, 2, 128, 8)), axis=2) < 64, 7, -7)
    a[:, 0, :, 127] = 7; a[:, 1, :, 127] = -7; a[:, 0, :, 0] = -7; a[:, 1, :, 0] = 7; a[:, :2, :, 50] = 7; a[:, :2, :, 81] = -7
    a[:, 2, :, 127] = 7; a[:, 2, :, 126] = -7; a[:, 2, :, 1] = 7; a[:, 2, :, 64] = -7
    return pack(v, z, a)
def setup_inputs_near(rng):
    v, z, a = plain(rng)
    cand = np.arange(60, 340); w = np.exp(-cand * 2.0 ** -13); off = np.abs(w - w.astype(np.float32).astype(BF).astype(np.float64))
    n = rng.choice(cand[np.argsort(-off)[:24]], 8)[:, None]
    mag = rng.integers(80, 112, (8, 16)); dif = (n // 16 + (np.arange(16)[None, :] < n % 16)) * rng.choice(np.array([-1, 1]), (8, 16))
    half = ((np.arange(8) // 2 + int(rng.integers(0, 2))) % 2 == 1)[:, None]
    far = half & (np.argsort(rng.random((8, 16)), axis=1) < 14); i = rng.integers(0, 25, (8, 16)); j = rng.integers(0, 8, (8, 16))
    one = np.where(far, (388 + 2 * i + 4 * j) * 2.0 ** -7, mag * 2.0 ** -6)
    two = np.where(far, (129 + 2 * i) * 2.0 ** -7, np.where(half, mag, mag + dif) * 2.0 ** -6)
    share = np.where(np.arange(8) % 2 == 0, 0.5, 0.1)[None, :, None, None]
    kind = rng.random((N, 8, 1, O)) < share
    v = np.where(kind, two[None, :, :, None], one[None, :, :, None])
    for g in np.flatnonzero(half): a[:, 1, :, 16 * g:16 * g + 16] = 0
    return pack(v, z, a)
def setup_inputs_corners(rng):
    v, z, a = plain(rng); sh = int(rng.integers(0, 8)); i16 = np.arange(16)
    for g in range(8):
        k = (g + sh) % 8; lo = 16 * g; hi = lo + 16; at = 16 * ((g + 3) % 8)
        if k == 0: v[:, g] = 0.25 + 0.0625 * v[:1, g, :, :1]
        elif k == 1: v[:, g] = 0.25
        elif k == 2: v[:, g] = np.where((rng.random((N, 1, O)) < 0.5) ^ (rng.random((1, 16, 1)) < 0.5), 1.0, 0.25)
        elif k == 3: v[:, g] = 0.25 + 0.1875 * v[:, g]; v[:, g, 1:] = 0.25
        else: v[:, g] = 1.0 + rng.random((N, 16, O))
        for q in range(N):
            c = (g + q + sh) % 8
            if c == 0: a[q, :2, :, lo:hi] = 0
            elif c == 1: a[q, :2, :, lo:hi] = a[q, :2, :, lo:lo + 1].copy()
            elif c == 2 or c == 3:
                a[q, :2, :, lo:hi] = 0
                for j in range(2): a[q, j, rng.integers(0, 128, 16), lo + i16] = -1 if c == 2 else 1
            elif c == 4: a[q, 0, :, lo:hi] = 0
            elif c == 5: a[q, 1, :, lo:hi] = 0
            elif c == 6:
                w = (1 + (q // 2) % (N - 1)) * (O // X)
                a[q, 0, :, lo:hi] = 0; a[q, 0, at:at + 16, lo:hi] = (w // 16 + (i16 < w % 16))[:, None]
            else:
                a[q, :2, :, lo:hi] = 0; a[q, 1, at:at + 12, lo:hi] = -7; a[q, 0, at + 12:at + 16, lo:hi] = -7
            e = (c + 3) % 8
            if e == 0: z[q, g] = 0
            elif e == 1: z[q, g] = 15
            elif e == 2: z[q, g] = rng.integers(7, 9, (16, O))
            elif e == 3: z[q, g] = rng.integers(0, 2, (16, O))
            elif e == 4:
                z[q, g] = 8
                if q % 2 == 1: z[q, g, :, S * int(rng.integers(0, Q)):][:, :S] = 0
            elif e == 5:
                nx = 8 * (np.arange(O) % X + q % 2) // 7; ny = 8 * (np.arange(O) // X + q % 2) // 7
                z[q, g, :12] = nx[None, :] // 12 + (np.arange(12)[:, None] < nx[None, :] % 12)
                z[q, g, 12:] = ny[None, :] // 4 + (np.arange(4)[:, None] < ny[None, :] % 4)
            b = (c + 6) % 8
            if b == 0: a[q, 2, :, lo:hi] = 0
            elif b == 1 or b == 2:
                a[q, 2, :, lo:hi] = 0; a[q, 2, rng.integers(0, 128, 16), lo + i16] = 1 if b == 1 else -1
            elif b == 3: a[q, 2, :, lo:hi] = 7
    return pack(v, z, a)
def setup_inputs_calm(rng):
    v, z, a = plain(rng); sh = int(rng.integers(0, 8)); i16 = np.arange(16); a[:, 2] = 0
    lev = np.ones(S)
    for t in range(R): lev[t % S] = 0.5 * lev[t % S] + 0.25 * np.mean(lev)
    v = 0.285 / np.sqrt(np.mean(lev * lev)) * (0.8 + 0.4 * rng.random((N, 8, 16, O)))
    s0, far = slip(); alike = float(rng.choice(s0[np.argsort(-far)[:6]]))
    owner = int(rng.integers(0, N)); pick = (np.arange(O) // S) % 16 == int(rng.integers(0, 16)); at = 16 * ((7 - sh) % 8); st = O // X
    for g in range(8):
        h = (g + sh) % 8; lo = 16 * g; hi = lo + 16
        for q in range(N): a[q, 2, lo + (i16 if h == 7 else rng.integers(0, 16, 16)), lo + i16] = 1 if h < 4 else 4
        u = rng.random((N, 16, O))
        if h < 4: z[:, g] = rng.integers(4 * h, 4 * h + 4, (N, 16, O))
        elif h < 6: z[:, g] = np.where(u < 0.0625, 15, np.where(u < 0.75, 14, 13))
        elif h == 6: z[:, g] = np.where(u < 0.01, 3, np.where(u < 0.03, 2, np.where(u < 0.08, 1, 0)))
        else: z[:, g] = 8 * ((i16[:, None] < 10) | pick[None, :])
        if h in (0, 1, 2, 7): a[:, :2, :, lo:hi] = 0
        for q in range(N):
            if h == 0:
                v[q, g] = 4.0 if q % 2 == 0 else 0.25
                if q % 2 == 1: a[q, 0, at + 10:at + 16, lo:hi] = (st // 6 + (np.arange(6) < st % 6))[:, None]
            elif h == 1:
                w = ((owner - q) % N) * st
                if 2 * w > Y: w = w - Y
                a[q, 0, at:at + 10, lo:hi] = (w // 10 + (np.arange(10) < w % 10))[:, None]
                a[q, 1, at:at + 10, lo:hi] = np.arange(10)[:, None] < (i16 % S)[None, :]
            elif h == 2 and q % 2 == 0:
                v[q, g] = alike; a[q, 1, at, lo:hi] = -1
    return pack(v, z, a)
def check_ranges(d):
    bad = []
    for k, lo, hi, w in (("v0", 0.25, 4, False), ("z0", 0, 15, True), ("ay", -7, 7, True), ("ax", -7, 7, True), ("bm", -7, 7, True)):
        a = np.asarray(d[k]).astype(np.float32)
        if not np.all((a >= lo) & (a <= hi)): bad.append("range of " + k)
        elif w and np.any(a != np.floor(a)): bad.append("whole numbers in " + k)
    return bad
def reference(v0, z0, ay, ax, bm):
    V = np.ascontiguousarray(v0.astype(np.float64).transpose(1, 0, 2)).reshape(8, 16, PL)
    z = np.ascontiguousarray(z0.astype(np.float32).astype(np.int64).transpose(1, 0, 2)).reshape(8, 16, PL)
    cy, cx, cb = [a.astype(np.float32).astype(np.int64).transpose(0, 2, 1) for a in (ay, ax, bm)]
    for t in range(R):
        nv = V.copy(); nz = z.copy()
        for r in range(N):
            own = r * O + S * np.arange(Q) + t % S
            zq = z.reshape(128, PL)[:, own]; vq = V[:, :, own]
            dy = np.matmul(cy[r], zq) >> 3; dx = np.matmul(cx[r], zq) >> 3
            pl = X * ((own // X + dy) & (Y - 1)) + ((own % X + dx) & (X - 1))
            ix = pl.reshape(8, 1, 16 * Q)
            m = np.max(np.take_along_axis(z, ix, 2).reshape(8, 16, 16, Q), axis=2).reshape(128, Q)
            nz[:, :, own] = ((np.matmul(cb[r], m) >> 2) & 15).reshape(8, 16, Q)
            vs = np.take_along_axis(V, ix, 2).reshape(8, 16, 16, Q)
            d = np.minimum(0.0078125 * np.sum(np.abs(vq[:, :, None, :] - vs), axis=1), 0.25)
            nv[:, :, own] = 0.5 * vq + 0.015625 * np.sum(np.exp(-d)[:, None] * vs, axis=2)
        V, z = nv, nz
    return {"yv": np.ascontiguousarray(V.reshape(128, N, O).transpose(1, 0, 2)).astype(np.float32), "yz": np.ascontiguousarray(z.reshape(128, N, O).transpose(1, 0, 2)).astype(np.float32)}

def check_inputs(d):
    bad = list(check_ranges(d))
    if not bad:
        for name, y in reference(**d).items():
            for q in range(N):
                v = np.abs(np.asarray(y[q], np.float64)); s = np.sqrt(np.mean(v * v))
                if v.max() > 5 * s or s < 2.0 ** -3: bad.append('%s of rank %d is uneven or too small' % (name, q))
    return bad

@@ -1,0 +1,506 @@
+from concourse.bass import DstId, RemoteDMATransfer
+from concourse.mybir import AluOpType, ActivationFunctionType
+
+ALU = AluOpType
+ACT = ActivationFunctionType
+Q, NCH, CQ = 512, 4, 128
+CW = 16 * CQ
+HW = CW // 2
+
+SCRATCH = {
+    "vin": ("sbuf", [128, 1024], "bfloat16"),
+    "zin": ("sbuf", [128, 1024], "bfloat16"),
+    "w0": ("sbuf", [128, 4096], "bfloat16"),
+    "w1": ("sbuf", [128, 6144], "float32"),
+    "zw": ("sbuf", [128, 8192], "bfloat16"),
+    "may": ("sbuf", [128, 128], "bfloat16"),
+    "mxx": ("sbuf", [128, 128], "bfloat16"),
+    "mbm": ("sbuf", [128, 128], "bfloat16"),
+    "ident": ("sbuf", [128, 128], "bfloat16"),
+    "idp": ("sbuf", [128, 128], "bfloat16"),
+    "idm": ("sbuf", [128, 128], "bfloat16"),
+    "ypos": ("sbuf", [128, Q], "bfloat16"),
+    "xpos": ("sbuf", [128, Q], "bfloat16"),
+    "fy": ("sbuf", [128, Q], "bfloat16"),
+    "fx": ("sbuf", [128, Q], "bfloat16"),
+    "y16": ("sbuf", [128, Q], "bfloat16"),
+    "x16": ("sbuf", [128, Q], "bfloat16"),
+    "x8": ("sbuf", [128, Q], "bfloat16"),
+    "off": ("sbuf", [128, 3 * Q], "uint16"),
+    "rep0": ("sbuf", [128, 16 * Q], "bfloat16"),
+    "rep1": ("sbuf", [128, 16 * Q], "bfloat16"),
+    "rep2": ("sbuf", [128, 16 * Q], "float32"),
+    "dd": ("sbuf", [128, 3 * CW], "float32"),
+    "aa": ("sbuf", [128, 2 * CW], "float32"),
+    "tt": ("sbuf", [128, CW], "float32"),
+    "tmp": ("sbuf", [128, CQ], "float32"),
+    "uu": ("sbuf", [128, 2 * CQ], "float32"),
+    "wt": ("sbuf", [128, 2 * CQ], "float32"),
+    "hi": ("sbuf", [128, 3 * 144], "bfloat16"),
+    "lo": ("sbuf", [128, 3 * 144], "float16"),
+    "sel": ("sbuf", [128, 2048], "bfloat16"),
+    "bo": ("sbuf", [128, 8], "float32"),
+    "shift": ("sbuf", [128, 128], "float32"),
+    "sumb": ("sbuf", [128, 16], "float32"),
+    "cz": ("sbuf", [128, 144], "bfloat16"),
+    "one": ("sbuf", [128, 128], "bfloat16"),
+    "zg": ("sbuf", [128, 16 * Q], "bfloat16"),
+    "zs": ("sbuf", [128, 2 * CW], "bfloat16"),
+    "zmask": ("sbuf", [128, CW], "bfloat16"),
+    "zi": ("sbuf", [128, Q], "int32"),
+    "yvs": ("sbuf", [128, 1024], "float32"),
+    "yzs": ("sbuf", [128, 1024], "float32"),
+    "pc0": ("psum", [128, 512], "float32"),
+    "pc1": ("psum", [128, 512], "float32"),
+    "pr0": ("psum", [128, 512], "float32"),
+    "pr1": ("psum", [128, 512], "float32"),
+    "pr2": ("psum", [128, 512], "float32"),
+    "pr3": ("psum", [128, 512], "float32"),
+    "pr4": ("psum", [128, 512], "float32"),
+    "pm": ("psum", [128, 512], "float32"),
+}
+MSGS = ["v0", "z0"] + ["v1c%d" % c for c in range(NCH)] + ["z1"] + ["v2c%d" % c for c in range(NCH)] + ["z2"]
+SEMAPHORES = (["cv", "ca", "cp", "cg", "ldv", "ldz", "ldm", "cast", "outs", "sent"]
+              + ["ar_" + s for s in ("v0", "z0", "v1", "z1", "v2", "z2")] + ["m_" + m for m in MSGS])
+
+
+def routes(T, topo):
+    cores = list(T.cores)
+    calls, arrivals = {}, {}
+
+    def add(src, msg, call):
+        calls.setdefault(src, {}).setdefault(msg, []).append(call)
+        for (_b, _c, _w, dst, eng, sem) in call:
+            arrivals[(dst, sem)] = arrivals.get((dst, sem), 0) + len(eng)
+
+    for r, me in enumerate(cores):
+        others = [c for c in cores if c != me]
+        peer = [c for c in others if topo.may_write(me, c)][0]
+        rest = [c for c in others if c != peer]
+        a = [c for c in rest if topo.host(c) == topo.host(me)][0]
+        b = [c for c in rest if c != a][0]
+        relays = [c for c in topo.cores_of(me) if c != me and topo.may_write(c, a) and topo.may_write(c, b)]
+        near = [c for c in relays if topo.die(c) == topo.die(me)]
+        far = [c for c in relays if topo.die(c) != topo.die(me)]
+        eoff = topo.engines(me, peer)
+        eon = topo.engines(me, relays[0])
+        erest = [e for e in eon if e not in eoff]
+        h, q = len(eoff) // 2, len(erest) // 2
+        n = 0
+        for msg in MSGS:
+            fin, hop = "ar_" + msg[:2], "m_" + msg
+            if msg in ("v0", "z0"):
+                buf = "w0" if msg == "v0" else "zw"
+                ce, co = Q * r, 2048 + Q * r
+                f0, f1, n0 = far[n % 2], far[(n + 1) % 2], near[n % 2]
+                add(me, msg, [(buf, ce, Q, f0, eoff, hop), (buf, co, Q, f1, erest[:q], hop), (buf, co, Q, n0, erest[q:], hop)])
+                add(me, msg, [(buf, ce, Q, peer, eoff[:h], fin), (buf, co, Q, peer, eoff[h:], fin)])
+                e = topo.engines(f0, a)
+                add(f0, msg, [(buf, ce, Q, a, e[:len(e) // 2], fin), (buf, ce, Q, b, e[len(e) // 2:], fin)])
+                add(f1, msg, [(buf, co, Q, b, topo.engines(f1, b), fin)])
+                add(n0, msg, [(buf, co, Q, a, topo.engines(n0, a), fin)])
+            else:
+                t = int(msg[1])
+                if msg[0] == "v":
+                    buf, col, w = "w1", 2048 * t + Q * r + CQ * int(msg[3]), CQ
+                else:
+                    buf, col, w = "zw", 2048 * (t + 1) + Q * r, Q
+                f0, n0 = far[n % 2], near[n % 2]
+                add(me, msg, [(buf, col, w, peer, eoff, fin), (buf, col, w, n0, erest[:q], hop), (buf, col, w, f0, erest[q:], hop)])
+                add(n0, msg, [(buf, col, w, a, topo.engines(n0, a), fin)])
+                add(f0, msg, [(buf, col, w, b, topo.engines(f0, b), fin)])
+            n += 1
+    return calls, arrivals
+
+
+def issue(g, core, T, topo, call):
+    trs, total = [], 0
+    for (buf, col, w, dst, eng, sem) in call:
+        rid, pid = topo.addr(dst, core)
+        m = 0
+        for e in eng:
+            m |= 1 << e
+        ap = T[buf][:, col:col + w]
+        trs.append(RemoteDMATransfer(dst_ids=[DstId(rid=rid, pnc=pid)], dma_engine_mask=m, remote_sem=T.sem[sem], src=ap, dst=ap))
+        total += len(eng)
+    g.remote_dma_fused(trs, local_sem=T.sem.sent)
+    return total
+
+
+def rank_program(g, core, T, topo):
+    calls, arrivals = routes(T, topo)
+    rank = T.rank_of(core)
+    if rank is None:
+        total = 0
+        for msg in MSGS:
+            for call in calls.get(core, {}).get(msg, []):
+                g.wait_ge(T.sem["m_" + msg], arrivals[(core, "m_" + msg)])
+                total += issue(g, core, T, topo, call)
+        if total:
+            g.wait_ge(T.sem.sent, total)
+        return
+
+    qs = {"v": g.vector, "a": g.scalar, "p": g.tensor, "g": g, "s": g.sync}
+    semof = {"v": "cv", "a": "ca", "p": "cp", "g": "cg"}
+    count = {"cv": 0, "ca": 0, "cp": 0, "cg": 0}
+    waited = {e: {} for e in qs}
+    wr, rd, bank = {}, {}, {}
+    sent = [0]
+
+    def wait(e, toks):
+        need = {}
+        for s, v in toks:
+            if v > waited[e].get(s, 0) and v > need.get(s, 0):
+                need[s] = v
+        for s, v in need.items():
+            qs[e].wait_ge(T.sem[s], v)
+            waited[e][s] = v
+
+    def deps(e, reads, writes, banks):
+        toks = []
+        for k in reads:
+            toks += wr.get(k, [])
+        for k in writes:
+            toks += wr.get(k, []) + rd.get(k, [])
+        for b in banks:
+            toks += [tk for (e2, tk) in bank.get(b, {}).items() if e2 != e]
+        if e == "p":
+            toks = [tk for tk in toks if tk[0] != "cp"]
+        wait(e, toks)
+
+    def mark(e, tok, reads, writes, banks):
+        for k in reads:
+            rd.setdefault(k, []).append(tok)
+        for k in writes:
+            wr[k] = [tok]
+            rd[k] = []
+        for b in banks:
+            bank.setdefault(b, {})[e] = tok
+
+    def op(e, fn, reads=(), writes=(), banks=()):
+        deps(e, reads, writes, banks)
+        s = semof[e]
+        count[s] += 1
+        fn().then_inc(T.sem[s], 1)
+        mark(e, (s, count[s]), reads, writes, banks)
+
+    def mms(lst, reads=(), writes=(), banks=()):
+        def fn():
+            for (o, l, r_, st, sp) in lst[:-1]:
+                g.tensor.matmul(o, l, r_, st, sp)
+            o, l, r_, st, sp = lst[-1]
+            return g.tensor.matmul(o, l, r_, st, sp)
+        op("p", fn, reads, writes, banks)
+
+    def send(msg, reads):
+        deps("g", reads, (), ())
+        for call in calls[core][msg]:
+            sent[0] += issue(g, core, T, topo, call)
+
+    def arrived(key, name):
+        wr.setdefault(key, []).append(("ar_" + name, arrivals[(core, "ar_" + name)]))
+
+    V, S = g.vector, g.scalar
+    own = Q * rank
+    pc = [T.pc0, T.pc1]
+    pr = [T.pr0, T.pr1, T.pr2, T.pr3, T.pr4]
+    rep = [T.rep0, T.rep1, T.rep2]
+    vwin = [T.w0[:, 0:4096], T.w1[:, 0:4096], T.w1[:, 2048:6144]]
+    vwin_keys = [["vE0", "vO0", "vin0"], ["cast", "vin1"] + [("vnew", 0, c) for c in range(NCH)],
+                 ["vin1", "vin2"] + [("vnew", t, c) for t in range(2) for c in range(NCH)]]
+    zwin_keys = [["zq0", "zq1", "zin0"], ["zq1", "zq2", "zin0", "zin1"], ["zq2", "zq3", "zin1", "zin2"]]
+    vq_keys = [["vE0"], ["vO0"], [("vnew", 0, c) for c in range(NCH)]]
+    for i, nm in enumerate(("v0", "v1", "v2")):
+        arrived("vin%d" % i, nm)
+    for i, nm in enumerate(("z0", "z1", "z2")):
+        arrived("zin%d" % i, nm)
+
+    def vq(t, a, b):
+        if t == 2:
+            return T.w1[:, 2048 + own + a:2048 + own + b]
+        return T.w0[:, 2048 * t + own + a:2048 * t + own + b]
+
+    g.sync.dma_start(T.vin[:], T.v0[:]).then_inc(T.sem.ldv, 16)
+    g.sync.dma_start(T.zin[:], T.z0[:]).then_inc(T.sem.ldz, 16)
+    g.sync.dma_start(T.may[:], T.ay[:]).then_inc(T.sem.ldm, 16)
+    g.sync.dma_start(T.mxx[:], T.ax[:]).then_inc(T.sem.ldm, 16)
+    g.sync.dma_start(T.mbm[:], T.bm[:]).then_inc(T.sem.ldm, 16)
+    wr["vin"], wr["zin"], wr["mats"] = [("ldv", 16)], [("ldz", 16)], [("ldm", 48)]
+
+    def fill(ap, val, key):
+        op("v", lambda: V.memset(ap, val), (), [key])
+
+    def select(ap, pattern, cmp, fillv, base, cm, key):
+        op("g", lambda: g.affine_select(ap, ap, pattern, cmp, fillv, base, cm), [key], [key])
+
+    fill(T.ident[:], 1.0, "ident")
+    op("g", lambda: g.iota(T.ypos[:], [[8, 32], [0, 16]], 256 * rank, 0, allow_small_or_imprecise_dtypes=True), (), ["ypos"])
+    select(T.ident[:], [[-1, 128]], ALU.is_equal, 0.0, 0, 1, "ident")
+    for j in range(16):
+        fill(T.xpos[:, j:Q:16], 16.0 * j, ("xpos", j))
+    fill(T.bo[:], 1.0, "bo")
+    fill(T.shift[:], 1.0, "shift")
+    fill(T.sumb[:], 1.0 / 64, "sumb")
+    fill(T.cz[0:32, :], 0.0, "cz")
+    fill(T.one[0:32, :], 1.0, "one")
+    fill(T.cz[0:1, 0:128:16], -128.0, "cz")
+    fill(T.cz[0:1, 128:144:2], 0.5, "cz")
+
+    op("v", lambda: V.tensor_copy(T.w0[:, own:own + Q], T.vin[:, 0:1024:2]), ["vin"], ["vE0"])
+    op("v", lambda: V.tensor_copy(T.w0[:, 2048 + own:2048 + own + Q], T.vin[:, 1:1024:2]), ["vin"], ["vO0"])
+    send("v0", ["vE0", "vO0"])
+    op("v", lambda: V.tensor_copy(T.zw[:, own:own + Q], T.zin[:, 0:1024:2]), ["zin"], ["zq0"])
+    op("v", lambda: V.tensor_copy(T.zw[:, 2048 + own:2048 + own + Q], T.zin[:, 1:1024:2]), ["zin"], ["zq1"])
+    send("z0", ["zq0", "zq1"])
+    op("v", lambda: V.tensor_scalar(T.idp[:], T.ident[:], 4096.0, None, ALU.mult), ["ident"], ["idp"])
+    op("v", lambda: V.tensor_scalar(T.idm[:], T.ident[:], -4096.0, None, ALU.mult), ["ident"], ["idm"])
+    fill(T.sel[:], 1.0, "sel")
+    select(T.bo[:], [[-16, 8]], ALU.is_ge, 0.0, 0, 1, "bo")
+    select(T.shift[:], [[-1, 128]], ALU.is_equal, 0.0, 1, 1, "shift")
+    select(T.sumb[:], [[-16, 8], [-15, 2]], ALU.is_ge, 0.0, 0, 1, "sumb")
+    select(T.bo[:], [[16, 8]], ALU.is_ge, 0.0, 15, -1, "bo")
+    select(T.shift[:], [[-1, 128]], ALU.not_equal, -1.0, 0, 1, "shift")
+    select(T.sumb[:], [[16, 8], [0, 2]], ALU.is_ge, 0.0, 15, -1, "sumb")
+    select(T.shift[:], [[0, 8], [1, 16]], ALU.is_gt, 0.0, 0, 0, "shift")
+    select(T.sel[:], [[-1, 128], [0, 16]], ALU.is_equal, 0.0, 0, 1, "sel")
+
+    xk = [("xpos", j) for j in range(16)]
+
+    def zq(t):
+        return T.zw[:, 2048 * t + own:2048 * t + own + Q]
+
+    def ident_act(out, in_, scale, bias, okey, b):
+        op("a", lambda: S.activation(out, in_, ACT.Identity, bias=float(bias), scale=float(scale)), [b], [okey], [b])
+
+    def list1(t):
+        k = ["mats", "ident", "zq%d" % t]
+        mms([(pr[0][:], T.may[:], zq(t), True, False), (pr[0][:], T.ident[:], T.ypos[:], False, True)], k + ["ypos"], ["r0"], ["r0"])
+        mms([(pr[1][:], T.mxx[:], zq(t), True, False), (pr[1][:], T.ident[:], T.xpos[:], False, True)], k + xk, ["r1"], ["r1"])
+        ident_act(T.fy[:], pr[0][:], -1, -196096.5, "fy", "r0")
+        ident_act(T.fx[:], pr[1][:], -1, -49024.5 - 8 * (t % 2), "fx", "r1")
+        mms([(pr[0][:], T.may[:], zq(t), True, False), (pr[0][:], T.ident[:], T.ypos[:], False, False),
+             (pr[0][:], T.ident[:], T.fy[:], False, True)], ["fy"], ["r0"], ["r0"])
+        mms([(pr[1][:], T.mxx[:], zq(t), True, False), (pr[1][:], T.ident[:], T.xpos[:], False, False),
+             (pr[1][:], T.ident[:], T.fx[:], False, True)], ["fx"], ["r1"], ["r1"])
+
+    def list2(t):
+        ident_act(T.y16[:], pr[0][:], 2, 393216 + 2057, "y16", "r0")
+
+    def list3(t):
+        s = 1 - 2 * (t % 2)
+        c = 8 * (t % 2) + 49152
+        ident_act(T.x16[:], pr[1][:], 1.0 / 16, c / 16 - 15.0 / 32 + 192, "x16", "r1")
+        ident_act(T.x8[:], pr[1][:], 256 * s, s * (256 * c + 392320), "x8", "r1")
+        big = T.idm if s > 0 else T.idp
+        mms([(T.pm[:], T.ident[:], T.y16[:], True, False), (T.pm[:], T.ident[:], T.x16[:], False, False),
+             (T.pm[:], big[:], T.x16[:], False, False), (T.pm[:], T.ident[:], T.x8[:], False, True)],
+            ["y16", "x16", "x8", "idp", "idm"], ["m"], ["m"])
+
+    def list4(t):
+        s = 1 - 2 * (t % 2)
+        c = -2064 - 192 * (1 - 4096 * s) - 2048 * 192 * s + (2048 if s < 0 else 0)
+        op("v", lambda: V.tensor_scalar(T.off[:, Q * t:Q * t + Q], T.pm[:], float(c), None, ALU.add), ["m"], [("off", t)], ["m"])
+
+    def repeat(t, k):
+        if t == 0:
+            op("v", lambda: V.tensor_copy(rep[0][:, k:16 * Q:16], vq(0, 0, Q)), vq_keys[0], [("rep", 0, k)])
+        else:
+            op("g", lambda: g.affine_select(rep[t][:, k:16 * Q:16], vq(t, 0, Q), [[0, Q]], ALU.is_ge, 0.0, 0, 0),
+               vq_keys[t], [("rep", t, k)])
+
+    list1(0)
+    list2(0)
+    list3(0)
+    for k in range(16):
+        repeat(0, k)
+    list4(0)
+    list1(1)
+    list2(1)
+    list3(1)
+    fill(T.zmask[:], 1.0, "zmask")
+    fill(T.zmask[:, 0:CW:16], 0.0, "zmask")
+    todo = [(1, k) for k in range(16)] + [(2, k) for k in range(16)]
+
+    def reps(n):
+        for _ in range(n):
+            repeat(*todo.pop(0))
+
+    reps(5)
+    deps("g", ["vO0", "vin0"], (), ())
+    g.dma_start(T.w1[:, 0:2048], T.w0[:, 2048:4096]).then_inc(T.sem.cast, 16)
+    wr["cast"] = [("cast", 16)]
+
+    outs = [0]
+    nb = [0]
+
+    def layer(t):
+        NB = (1, 2, 1)
+        grp_of_piece = (0, 0, 1, 1, 1, 1, 2, 2)
+        first_piece = (0, 2, 6)
+
+        def dg(p):
+            o, a = HW * (p % 6), HW * p
+            f = Q * t + a // 16
+            op("v", lambda: V.tensor_tensor(T.dd[:, o:o + HW], vwin[t].indirect(T.off[:, f:f + HW // 16]), rep[t][:, a:a + HW], ALU.subtract),
+               vwin_keys[t] + [("off", t)] + [("rep", t, k) for k in range(16)], [("d", p % 6)])
+
+        def ab(p):
+            o, a = HW * (p % 6), HW * (p % 4)
+            op("a", lambda: S.activation(T.aa[:, a:a + HW], T.dd[:, o:o + HW], ACT.Abs), [("d", p % 6)], [("a", p % 4)])
+
+        def smm(p):
+            c = grp_of_piece[p]
+            a, lst = HW * (p % 4), []
+            for i in range(8):
+                n = 8 * (p - first_piece[c]) + i
+                o = 128 * (n % NB[c]) + 8 * (n // NB[c])
+                lst.append((pc[c % 2][:, o:o + 8], T.aa[:, a + 128 * i:a + 128 * i + 128], T.bo[:], True, True))
+            mms(lst, [("a", p % 4), "bo"], [], [("c", c % 2)])
+
+        def clamp(c):
+            n, b = 128 * NB[c], pc[c % 2]
+            op("a", lambda: S.activation(T.uu[:, 0:n], b[:, 0:n], ACT.Relu, bias=0.25, scale=-1.0 / 128), (), ["u"], [("c", c % 2)])
+            lst = []
+            for i in range(NB[c]):
+                o = b[:, 128 * i:128 * i + 128]
+                lst += [(o, T.uu[:, 128 * i:128 * i + 128], T.shift[:], True, False), (o, T.one[0:1, :], T.cz[0:1, 0:128], False, True)]
+            mms(lst, ["u", "shift", "one", "cz"], [], [("c", c % 2)])
+            op("a", lambda: S.activation(T.wt[:, 0:n], T.uu[:, 0:n], ACT.Exp, bias=-0.25), ["u"], ["w"])
+            lst = []
+            for i in range(NB[c]):
+                o = b[:, n + 16 * i:n + 16 * i + 16]
+                lst += [(o, T.wt[:, 128 * i:128 * i + 128], T.sumb[:], True, False), (o, T.one[0:1, :], T.cz[0:1, 128:144], False, True)]
+            mms(lst, ["w", "sumb"], [], [("c", c % 2)])
+
+        def ratio(c):
+            n, m, b, h = 128 * NB[c], 144 * NB[c], pc[c % 2], 144 * (c % 2)
+            op("a", lambda: S.activation(b[:, 0:n], b[:, 0:n], ACT.Exp), (), [("x", c % 2)], [("c", c % 2)])
+            op("a", lambda: S.activation(T.hi[:, h:h + m], b[:, 0:m], ACT.Copy), [("x", c % 2)], [("hi", c % 2)], [("c", c % 2)])
+
+        def low(c):
+            m, b, h = 144 * NB[c], pc[c % 2], 144 * (c % 2)
+            op("v", lambda: V.tensor_tensor(T.lo[:, h:h + m], b[:, 0:m], T.hi[:, h:h + m], ALU.subtract),
+               [("hi", c % 2)], [("lo", c % 2)], [("c", c % 2)])
+
+        held = {}
+
+        def bc(u):
+            c = grp_of_piece[u // 2]
+            n = nb[0] % 5
+            nb[0] += 1
+            held[u] = n
+            w, h, per = 128 * NB[c], 144 * (c % 2), 4 // NB[c]
+            lst = []
+            for i in range(per):
+                s0 = 128 * (per * (u - 2 * first_piece[c]) + i)
+                o = pr[n][:, w * i:w * i + w]
+                lst.append((o, T.sel[:, s0:s0 + 128], T.hi[:, h:h + w], True, False))
+                lst.append((o, T.sel[:, s0:s0 + 128], T.lo[:, h:h + w], False, True))
+            mms(lst, [("hi", c % 2), ("lo", c % 2), "sel"], [], ["r%d" % n])
+
+        def scan(u):
+            n = held[u]
+            o, b = 512 * (u % 12), u % 4
+            op("v", lambda: V.tensor_tensor_scan(T.tt[:, 512 * b:512 * b + 512], pr[n][:], T.dd[:, o:o + 512], 0.0, ALU.mult, ALU.add),
+               [("d", (u // 2) % 6)], [("t", b)], ["r%d" % n])
+
+        def abmm(c):
+            w, h = 16 * NB[c], 144 * (c % 2) + 128 * NB[c]
+            lst = []
+            for i in range(16):
+                o = pc[c % 2][:, w * i:w * i + w]
+                lst.append((o, T.sel[:, 128 * i:128 * i + 128], T.hi[:, h:h + w], True, False))
+                lst.append((o, T.sel[:, 128 * i:128 * i + 128], T.lo[:, h:h + w], False, True))
+            mms(lst, [("hi", c % 2), ("lo", c % 2), "sel"], [], [("c", c % 2)])
+
+        def fin(c):
+            bk, o0 = (0, 1, 1, 0)[c], (0, 0, 256, 0)[c]
+            pa, pb = pc[bk][:, o0:o0 + 256:2], pc[bk][:, o0 + 1:o0 + 256:2]
+            op("v", lambda: V.tensor_tensor(pa, vq(t, CQ * c, CQ * c + CQ), pa, ALU.mult), vq_keys[t], [("pa", c)], [("c", bk)])
+            op("v", lambda: V.tensor_tensor(T.tmp[:], T.tt[:, 15:CW:16], pb, ALU.mult), [("t", b) for b in range(4)], ["tmp"], [("c", bk)])
+            if t < 2:
+                o = 2048 * (t + 1) + own + CQ * c
+                dst = T.w1[:, o:o + CQ]
+            else:
+                dst = T.yvs[:, 2 * CQ * c:2 * CQ * (c + 1):2]
+            op("v", lambda: V.tensor_tensor(dst, T.tmp[:], pa, ALU.add), ["tmp", ("pa", c)], [("vnew", t, c)], [("c", bk)])
+            if t < 2:
+                send("v%dc%d" % (t + 1, c), [("vnew", t, c)])
+            else:
+                deps("s", [("vnew", t, c), "yvodd"], (), ())
+                g.sync.dma_start(T.yv[:, 2 * CQ * c:2 * CQ * (c + 1)], T.yvs[:, 2 * CQ * c:2 * CQ * (c + 1)]).then_inc(T.sem.outs, 16)
+                outs[0] += 16
+
+        zp = [0]
+
+        def zg(n):
+            for _ in range(n):
+                p = zp[0]
+                zp[0] += 1
+                op("a", lambda: S.activation(T.zg[:, 512 * p:512 * p + 512],
+                                             T.zw[:, 2048 * t:2048 * t + 4096].indirect(T.off[:, Q * t + 32 * p:Q * t + 32 * p + 32]), ACT.Copy),
+                   zwin_keys[t] + [("off", t)], [("zg", p)])
+
+        def zmax(c):
+            o = CW * (c % 2)
+            op("v", lambda: V.tensor_tensor_scan(T.zs[:, o:o + CW], T.zmask[:], T.zg[:, CW * c:CW * c + CW], 0.0, ALU.mult, ALU.max),
+               ["zmask"] + [("zg", 4 * c + i) for i in range(4)], [("zs", c % 2)])
+            mms([(T.pm[:, CQ * c:CQ * c + CQ], T.mbm[:], T.zs[:, o + 15:o + CW:16], True, True)], [("zs", c % 2), "mats"], [], ["m"])
+
+        def znew(a, b):
+            zi = T.zi[:, a:b]
+            op("v", lambda: V.tensor_copy(zi, T.pm[:, a:b]), (), ["zi"], ["m"])
+            op("v", lambda: V.tensor_scalar(zi, zi, 2, 15, ALU.arith_shift_right, ALU.bitwise_and), ["zi"], ["zi"])
+            if t < 2:
+                o = 2048 * (t + 2) + own
+                op("v", lambda: V.tensor_copy(T.zw[:, o + a:o + b], zi), ["zi"], ["zq%d" % (t + 2)])
+                if b == Q:
+                    send("z%d" % (t + 1), ["zq%d" % (t + 2)])
+            else:
+                op("v", lambda: V.tensor_copy(T.yzs[:, 2 * a:2 * b:2], zi), ["zi"], ["yzeven"])
+                deps("s", ["yzeven", "yzodd"], (), ())
+                g.sync.dma_start(T.yz[:, 2 * a:2 * b], T.yzs[:, 2 * a:2 * b]).then_inc(T.sem.outs, 16)
+                outs[0] += 16
+
+        def early(i):
+            if t == 1:
+                (list1, list2, list3)[i](2)
+            if t == 2 and i == 0:
+                op("a", lambda: S.activation(T.yzs[:, 1:1024:2], zq(3), ACT.Copy), ["zq3"], ["yzodd"])
+                o = 4096 + own
+                op("g", lambda: g.affine_select(T.yvs[:, 1:1024:2], T.w1[:, o:o + Q], [[0, Q]], ALU.is_ge, 0.0, 0, 0),
+                   [("vnew", 1, c) for c in range(NCH)], ["yvodd"])
+
+        nrep = ((5, 3, 2, 1), (8, 3, 2, 0), (0, 0, 0, 0))[t]
+        dg(0); early(0); ab(0); smm(0)
+        dg(1); early(1); ab(1); smm(1)
+        dg(2); early(2); clamp(0); ab(2); ratio(0); smm(2)
+        dg(3); ab(3); smm(3)
+        dg(4); low(0); ab(4); bc(0); bc(1); smm(4); bc(2); bc(3)
+        dg(5); ab(5); smm(5); abmm(0)
+        scan(0); scan(1); scan(2); scan(3)
+        clamp(1); zg(2); ratio(1)
+        reps(nrep[0]); fin(0)
+        dg(6); low(1); zg(1); ab(6); bc(4); bc(5); smm(6); bc(6); bc(7)
+        dg(7); zg(1); ab(7); bc(8); smm(7); abmm(1)
+        scan(4); bc(9); scan(5)
+        zg(1); clamp(2); zg(1); ratio(2)
+        bc(10); scan(6); bc(11); scan(7)
+        reps(nrep[1]); fin(1)
+        scan(8); low(2); bc(12); scan(9); bc(13); scan(10); bc(14); scan(11); bc(15); abmm(2)
+        reps(nrep[2]); fin(2)
+        scan(12); scan(13); scan(14); scan(15); fin(3)
+        reps(nrep[3])
+        zg(10)
+        if t < 2:
+            list4(t + 1)
+        if t == 0:
+            reps(3)
+        zmax(0); zmax(1); zmax(2); znew(0, 3 * CQ); zmax(3); znew(3 * CQ, Q)
+
+    for t in range(3):
+        layer(t)
+
+    g.wait_ge(T.sem.sent, sent[0])
+    wait("s", [(s, v) for s, v in count.items()])
+    g.sync.wait_ge(T.sem.outs, outs[0])

@@ -1,11 +1,21 @@
+import math
 from concourse.bass import DstId, RemoteDMATransfer
 from concourse.mybir import AluOpType, ActivationFunctionType
 
 ALU = AluOpType
 ACT = ActivationFunctionType
-Q, NCH, CQ = 512, 4, 128
+Q, CQ = 512, 128
 CW = 16 * CQ
-HW = CW // 2
+PW = CW // 2
+GROUPS = (1, 2, 1)
+FINS = ((0, 128), (128, 384), (384, 512))
+BY_SCALAR = (4, 5)
+ZHALF = ((0, 256), (256, 512))
+ORDER = """dg4 dg0 dg5 dg1 ab0 rep0 rep1 sm0 dg2 ab1 dg3 ab2 sm1 relu0 sm2 expw0 -za1 ab3 -zb1 -zc1 list0 diff0 sumw0 expr0 sm3 high0
+ab4 low0 dg6 rep2 ab5 dg7 abm0 bc0 sm4 ab6 sm5 rep3 aside0 relu1 bc1 expw1 bc2 diff1 bc3 sumw1 SCAN0 ab7 SCAN1 expr1 rep4 high1
+sm6 sm7 low1 self0 zg0 scale0 bc4 bc5 fin0 bc6 SCAN2 rep5 bc7 relu2 expw2 sumw2 bc8 SCAN3 bc9 bc10 bc11 SCAN4 zg1 diff2 expr2
+abm1 high2 SCAN5 rep6 low2 self1 scale1 bc12 bc13 fin1 SCAN6 bc14 bc15 abm2 zg2 zg3 zg4 SCAN7 rep7 list1 self2 scale2 fin2
+zmax0 zmax1 zg5 list2 list3 zv7 zg6 za0 zmax2 zb0 list4 zmax3 zc0"""
 
 SCRATCH = {
     "vin": ("sbuf", [128, 1024], "bfloat16"),
@@ -30,14 +40,13 @@ SCRATCH = {
     "rep0": ("sbuf", [128, 16 * Q], "bfloat16"),
     "rep1": ("sbuf", [128, 16 * Q], "bfloat16"),
     "rep2": ("sbuf", [128, 16 * Q], "float32"),
-    "dd": ("sbuf", [128, 3 * CW], "float32"),
-    "aa": ("sbuf", [128, 2 * CW], "float32"),
-    "tt": ("sbuf", [128, CW], "float32"),
-    "tmp": ("sbuf", [128, CQ], "float32"),
-    "uu": ("sbuf", [128, 2 * CQ], "float32"),
-    "wt": ("sbuf", [128, 2 * CQ], "float32"),
-    "hi": ("sbuf", [128, 3 * 144], "bfloat16"),
-    "lo": ("sbuf", [128, 3 * 144], "float16"),
+    "dd": ("sbuf", [128, 5 * CW], "float32"),
+    "aa": ("sbuf", [128, 4 * PW], "float32"),
+    "tmp": ("sbuf", [128, 4 * CQ], "float32"),
+    "uu": ("sbuf", [128, Q], "float32"),
+    "wt": ("sbuf", [128, Q], "float32"),
+    "hi": ("sbuf", [128, 4 * 144], "bfloat16"),
+    "lo": ("sbuf", [128, 4 * 144], "float16"),
     "sel": ("sbuf", [128, 2048], "bfloat16"),
     "bo": ("sbuf", [128, 8], "float32"),
     "shift": ("sbuf", [128, 128], "float32"),
@@ -52,16 +61,15 @@ SCRATCH = {
     "yzs": ("sbuf", [128, 1024], "float32"),
     "pc0": ("psum", [128, 512], "float32"),
     "pc1": ("psum", [128, 512], "float32"),
-    "pr0": ("psum", [128, 512], "float32"),
-    "pr1": ("psum", [128, 512], "float32"),
-    "pr2": ("psum", [128, 512], "float32"),
-    "pr3": ("psum", [128, 512], "float32"),
-    "pr4": ("psum", [128, 512], "float32"),
-    "pm": ("psum", [128, 512], "float32"),
+    "pr0": ("psum", [128, 1024], "float32"),
+    "pr1": ("psum", [128, 1024], "float32"),
+    "pr2": ("psum", [128, 1024], "float32"),
 }
-MSGS = ["v0", "z0"] + ["v1c%d" % c for c in range(NCH)] + ["z1"] + ["v2c%d" % c for c in range(NCH)] + ["z2"]
+MSGS = (["v0e", "v0o", "v0p", "z0e", "z0o", "z0p"] + ["v1c%d" % c for c in range(len(FINS))] + ["z1c0", "z1c1"]
+        + ["v2c%d" % c for c in range(len(FINS))] + ["z2c0", "z2c1"])
 SEMAPHORES = (["cv", "ca", "cp", "cg", "ldv", "ldz", "ldm", "cast", "outs", "sent"]
-              + ["ar_" + s for s in ("v0", "z0", "v1", "z1", "v2", "z2")] + ["m_" + m for m in MSGS])
+              + ["ar_" + s for s in ("v0", "z0", "v1", "z1", "v2", "z2")] + ["m_" + m for m in MSGS]
+              + ["add%d_%d" % (t, p) for t in range(3) for p in range(8)])
 
 
 def routes(T, topo):
@@ -73,6 +81,7 @@ def routes(T, topo):
         for (_b, _c, _w, dst, eng, sem) in call:
             arrivals[(dst, sem)] = arrivals.get((dst, sem), 0) + len(eng)
 
+    world = range(max(topo.cores_of(max(cores))) + 1 + len(topo.cores_of(cores[0])))
     for r, me in enumerate(cores):
         others = [c for c in cores if c != me]
         peer = [c for c in others if topo.may_write(me, c)][0]
@@ -82,34 +91,40 @@ def routes(T, topo):
         relays = [c for c in topo.cores_of(me) if c != me and topo.may_write(c, a) and topo.may_write(c, b)]
         near = [c for c in relays if topo.die(c) == topo.die(me)]
         far = [c for c in relays if topo.die(c) != topo.die(me)]
+        mate = [c for c in world if topo.mates(c, a) and topo.may_write(c, a) and topo.may_write(me, c)]
+        mate = [[c for c in mate if topo.die(c) == d][0] for d in sorted(set(topo.die(c) for c in mate))]
         eoff = topo.engines(me, peer)
-        eon = topo.engines(me, relays[0])
-        erest = [e for e in eon if e not in eoff]
-        h, q = len(eoff) // 2, len(erest) // 2
-        n = 0
-        for msg in MSGS:
+        erest = [e for e in topo.engines(me, relays[0]) if e not in eoff]
+        h = len(eoff) // 2
+        for n, msg in enumerate(MSGS):
             fin, hop = "ar_" + msg[:2], "m_" + msg
-            if msg in ("v0", "z0"):
-                buf = "w0" if msg == "v0" else "zw"
+            if msg[1] == "0":
+                buf = "w0" if msg[0] == "v" else "zw"
                 ce, co = Q * r, 2048 + Q * r
-                f0, f1, n0 = far[n % 2], far[(n + 1) % 2], near[n % 2]
-                add(me, msg, [(buf, ce, Q, f0, eoff, hop), (buf, co, Q, f1, erest[:q], hop), (buf, co, Q, n0, erest[q:], hop)])
-                add(me, msg, [(buf, ce, Q, peer, eoff[:h], fin), (buf, co, Q, peer, eoff[h:], fin)])
-                e = topo.engines(f0, a)
-                add(f0, msg, [(buf, ce, Q, a, e[:len(e) // 2], fin), (buf, ce, Q, b, e[len(e) // 2:], fin)])
-                add(f1, msg, [(buf, co, Q, b, topo.engines(f1, b), fin)])
-                add(n0, msg, [(buf, co, Q, a, topo.engines(n0, a), fin)])
+                if msg[2] == "p":
+                    add(me, msg, [(buf, ce, Q, peer, eoff[:h], fin), (buf, co, Q, peer, eoff[h:], fin)])
+                else:
+                    i = "eo".index(msg[2])
+                    col, mine = (ce, co)[i], (far[0], near[0])[i]
+                    add(me, msg, [(buf, col, Q, mate[i], eoff, hop), (buf, col, Q, mine, erest, hop)])
+                    add(mate[i], msg, [(buf, col, Q, a, topo.engines(mate[i], a), fin)])
+                    add(mine, msg, [(buf, col, Q, b, topo.engines(mine, b), fin)])
             else:
                 t = int(msg[1])
                 if msg[0] == "v":
-                    buf, col, w = "w1", 2048 * t + Q * r + CQ * int(msg[3]), CQ
+                    q0, q1 = FINS[int(msg[3])]
+                    buf, col, w = "w1", 2048 * t + Q * r + q0, q1 - q0
                 else:
-                    buf, col, w = "zw", 2048 * (t + 1) + Q * r, Q
+                    q0, q1 = ZHALF[int(msg[3])]
+                    buf, col, w = "zw", 2048 * (t + 1) + Q * r + q0, q1 - q0
                 f0, n0 = far[n % 2], near[n % 2]
-                add(me, msg, [(buf, col, w, peer, eoff, fin), (buf, col, w, n0, erest[:q], hop), (buf, col, w, f0, erest[q:], hop)])
+                if q1 == Q:
+                    add(me, msg, [(buf, col, w, n0, eoff, hop), (buf, col, w, f0, erest, hop)])
+                    add(me, msg, [(buf, col, w, peer, eoff, fin)])
+                else:
+                    add(me, msg, [(buf, col, w, peer, eoff, fin), (buf, col, w, n0, erest[:h], hop), (buf, col, w, f0, erest[h:], hop)])
                 add(n0, msg, [(buf, col, w, a, topo.engines(n0, a), fin)])
                 add(f0, msg, [(buf, col, w, b, topo.engines(f0, b), fin)])
-            n += 1
     return calls, arrivals
 
 
@@ -148,11 +163,11 @@ def rank_program(g, core, T, topo):
     sent = [0]
 
     def wait(e, toks):
-        need = {}
+        most = {}
         for s, v in toks:
-            if v > waited[e].get(s, 0) and v > need.get(s, 0):
-                need[s] = v
-        for s, v in need.items():
+            if v > waited[e].get(s, 0) and v > most.get(s, 0):
+                most[s] = v
+        for s, v in most.items():
             qs[e].wait_ge(T.sem[s], v)
             waited[e][s] = v
 
@@ -168,7 +183,12 @@ def rank_program(g, core, T, topo):
             toks = [tk for tk in toks if tk[0] != "cp"]
         wait(e, toks)
 
-    def mark(e, tok, reads, writes, banks):
+    def op(e, fn, reads=(), writes=(), banks=()):
+        deps(e, reads, writes, banks)
+        s = semof[e]
+        count[s] += 1
+        fn().then_inc(T.sem[s], 1)
+        tok = (s, count[s])
         for k in reads:
             rd.setdefault(k, []).append(tok)
         for k in writes:
@@ -176,13 +196,6 @@ def rank_program(g, core, T, topo):
             rd[k] = []
         for b in banks:
             bank.setdefault(b, {})[e] = tok
-
-    def op(e, fn, reads=(), writes=(), banks=()):
-        deps(e, reads, writes, banks)
-        s = semof[e]
-        count[s] += 1
-        fn().then_inc(T.sem[s], 1)
-        mark(e, (s, count[s]), reads, writes, banks)
 
     def mms(lst, reads=(), writes=(), banks=()):
         def fn():
@@ -197,23 +210,21 @@ def rank_program(g, core, T, topo):
         for call in calls[core][msg]:
             sent[0] += issue(g, core, T, topo, call)
 
-    def arrived(key, name):
-        wr.setdefault(key, []).append(("ar_" + name, arrivals[(core, "ar_" + name)]))
-
     V, S = g.vector, g.scalar
     own = Q * rank
     pc = [T.pc0, T.pc1]
-    pr = [T.pr0, T.pr1, T.pr2, T.pr3, T.pr4]
+    pair = [T.pr0, T.pr1, T.pr2]
+    pr = [b[:, o:o + 512] for b in pair for o in (0, 512)]
     rep = [T.rep0, T.rep1, T.rep2]
+    vnew = [[("vnew", t, c) for c in range(len(FINS))] for t in range(3)]
     vwin = [T.w0[:, 0:4096], T.w1[:, 0:4096], T.w1[:, 2048:6144]]
-    vwin_keys = [["vE0", "vO0", "vin0"], ["cast", "vin1"] + [("vnew", 0, c) for c in range(NCH)],
-                 ["vin1", "vin2"] + [("vnew", t, c) for t in range(2) for c in range(NCH)]]
+    vwin_keys = [["vE0", "vO0", "vin0"], ["cast", "vin1"] + vnew[0], ["vin1", "vin2"] + vnew[0] + vnew[1]]
     zwin_keys = [["zq0", "zq1", "zin0"], ["zq1", "zq2", "zin0", "zin1"], ["zq2", "zq3", "zin1", "zin2"]]
-    vq_keys = [["vE0"], ["vO0"], [("vnew", 0, c) for c in range(NCH)]]
-    for i, nm in enumerate(("v0", "v1", "v2")):
-        arrived("vin%d" % i, nm)
-    for i, nm in enumerate(("z0", "z1", "z2")):
-        arrived("zin%d" % i, nm)
+    vq_keys = [["vE0"], ["vO0"], vnew[0]]
+    for kind in "vz":
+        for i in range(3):
+            s = "ar_%s%d" % (kind, i)
+            wr["%sin%d" % (kind, i)] = [(s, arrivals[(core, s)])]
 
     def vq(t, a, b):
         if t == 2:
@@ -236,22 +247,20 @@ def rank_program(g, core, T, topo):
     fill(T.ident[:], 1.0, "ident")
     op("g", lambda: g.iota(T.ypos[:], [[8, 32], [0, 16]], 256 * rank, 0, allow_small_or_imprecise_dtypes=True), (), ["ypos"])
     select(T.ident[:], [[-1, 128]], ALU.is_equal, 0.0, 0, 1, "ident")
-    for j in range(16):
-        fill(T.xpos[:, j:Q:16], 16.0 * j, ("xpos", j))
     fill(T.bo[:], 1.0, "bo")
     fill(T.shift[:], 1.0, "shift")
-    fill(T.sumb[:], 1.0 / 64, "sumb")
-    fill(T.cz[0:32, :], 0.0, "cz")
-    fill(T.one[0:32, :], 1.0, "one")
-    fill(T.cz[0:1, 0:128:16], -128.0, "cz")
-    fill(T.cz[0:1, 128:144:2], 0.5, "cz")
+    fill(T.sumb[:], -0.25 - math.log(64.0), "sumb")
+    op("a", lambda: S.activation(T.sumb[:], T.sumb[:], ACT.Exp), ["sumb"], ["sumb"])
+    for j in range(16):
+        fill(T.xpos[:, j:Q:16], 16.0 * j, ("xpos", j))
 
     op("v", lambda: V.tensor_copy(T.w0[:, own:own + Q], T.vin[:, 0:1024:2]), ["vin"], ["vE0"])
+    send("v0e", ["vE0"])
     op("v", lambda: V.tensor_copy(T.w0[:, 2048 + own:2048 + own + Q], T.vin[:, 1:1024:2]), ["vin"], ["vO0"])
-    send("v0", ["vE0", "vO0"])
+    send("v0o", ["vO0"])
+    send("v0p", ["vE0", "vO0"])
     op("v", lambda: V.tensor_copy(T.zw[:, own:own + Q], T.zin[:, 0:1024:2]), ["zin"], ["zq0"])
     op("v", lambda: V.tensor_copy(T.zw[:, 2048 + own:2048 + own + Q], T.zin[:, 1:1024:2]), ["zin"], ["zq1"])
-    send("z0", ["zq0", "zq1"])
     op("v", lambda: V.tensor_scalar(T.idp[:], T.ident[:], 4096.0, None, ALU.mult), ["ident"], ["idp"])
     op("v", lambda: V.tensor_scalar(T.idm[:], T.ident[:], -4096.0, None, ALU.mult), ["ident"], ["idm"])
     fill(T.sel[:], 1.0, "sel")
@@ -265,241 +274,357 @@ def rank_program(g, core, T, topo):
     select(T.sel[:], [[-1, 128], [0, 16]], ALU.is_equal, 0.0, 0, 1, "sel")
 
     xk = [("xpos", j) for j in range(16)]
+    holder, done = {}, set()
+
+    def need(*names):
+        for n in names:
+            assert n in done, n
+
+    def take(who, n):
+        assert holder.get(n) is None
+        holder[n] = who
+        return n
 
     def zq(t):
         return T.zw[:, 2048 * t + own:2048 * t + own + Q]
 
-    def ident_act(out, in_, scale, bias, okey, b):
-        op("a", lambda: S.activation(out, in_, ACT.Identity, bias=float(bias), scale=float(scale)), [b], [okey], [b])
+    def ident_act(out, n, scale, bias, okey):
+        b = "r%d" % n
+        op("a", lambda: S.activation(out, pr[n], ACT.Identity, bias=float(bias), scale=float(scale)), [b], [okey], [b])
+
+    BY, BX, BM = 0, 2, 4
 
     def list1(t):
         k = ["mats", "ident", "zq%d" % t]
-        mms([(pr[0][:], T.may[:], zq(t), True, False), (pr[0][:], T.ident[:], T.ypos[:], False, True)], k + ["ypos"], ["r0"], ["r0"])
-        mms([(pr[1][:], T.mxx[:], zq(t), True, False), (pr[1][:], T.ident[:], T.xpos[:], False, True)], k + xk, ["r1"], ["r1"])
-        ident_act(T.fy[:], pr[0][:], -1, -196096.5, "fy", "r0")
-        ident_act(T.fx[:], pr[1][:], -1, -49024.5 - 8 * (t % 2), "fx", "r1")
-        mms([(pr[0][:], T.may[:], zq(t), True, False), (pr[0][:], T.ident[:], T.ypos[:], False, False),
-             (pr[0][:], T.ident[:], T.fy[:], False, True)], ["fy"], ["r0"], ["r0"])
-        mms([(pr[1][:], T.mxx[:], zq(t), True, False), (pr[1][:], T.ident[:], T.xpos[:], False, False),
-             (pr[1][:], T.ident[:], T.fx[:], False, True)], ["fx"], ["r1"], ["r1"])
+        take("y", BY)
+        take("x", BX)
+        for n, m, pos, pk in ((BY, T.may, T.ypos, ["ypos"]), (BX, T.mxx, T.xpos, xk)):
+            mms([(pr[n], m[:], zq(t), True, False), (pr[n], T.ident[:], pos[:], False, True)], k + pk, ["r%d" % n], ["r%d" % n])
+        ident_act(T.fy[:], BY, -1, -196096.5, "fy")
+        ident_act(T.fx[:], BX, -1, -49024.5 - 8 * (t % 2), "fx")
+        for n, m, pos, f, fk in ((BY, T.may, T.ypos, T.fy, "fy"), (BX, T.mxx, T.xpos, T.fx, "fx")):
+            mms([(pr[n], m[:], zq(t), True, False), (pr[n], T.ident[:], pos[:], False, False),
+                 (pr[n], T.ident[:], f[:], False, True)], [fk], ["r%d" % n], ["r%d" % n])
 
     def list2(t):
-        ident_act(T.y16[:], pr[0][:], 2, 393216 + 2057, "y16", "r0")
+        ident_act(T.y16[:], BY, 2, 393216 + 2057, "y16")
+        holder[BY] = None
 
     def list3(t):
         s = 1 - 2 * (t % 2)
         c = 8 * (t % 2) + 49152
-        ident_act(T.x16[:], pr[1][:], 1.0 / 16, c / 16 - 15.0 / 32 + 192, "x16", "r1")
-        ident_act(T.x8[:], pr[1][:], 256 * s, s * (256 * c + 392320), "x8", "r1")
+        ident_act(T.x16[:], BX, 1.0 / 16, c / 16 - 15.0 / 32 + 192, "x16")
+        ident_act(T.x8[:], BX, 256 * s, s * (256 * c + 392320), "x8")
+        holder[BX] = None
         big = T.idm if s > 0 else T.idp
-        mms([(T.pm[:], T.ident[:], T.y16[:], True, False), (T.pm[:], T.ident[:], T.x16[:], False, False),
-             (T.pm[:], big[:], T.x16[:], False, False), (T.pm[:], T.ident[:], T.x8[:], False, True)],
-            ["y16", "x16", "x8", "idp", "idm"], ["m"], ["m"])
+        pm = pr[take("m", BM)]
+        mms([(pm, T.ident[:], T.y16[:], True, False), (pm, T.ident[:], T.x16[:], False, False),
+             (pm, big[:], T.x16[:], False, False), (pm, T.ident[:], T.x8[:], False, True)],
+            ["y16", "x16", "x8", "idp", "idm"], ["r%d" % BM], ["r%d" % BM])
 
     def list4(t):
         s = 1 - 2 * (t % 2)
         c = -2064 - 192 * (1 - 4096 * s) - 2048 * 192 * s + (2048 if s < 0 else 0)
-        op("v", lambda: V.tensor_scalar(T.off[:, Q * t:Q * t + Q], T.pm[:], float(c), None, ALU.add), ["m"], [("off", t)], ["m"])
+        op("v", lambda: V.tensor_scalar(T.off[:, Q * t:Q * t + Q], pr[BM], float(c), None, ALU.add), ["r%d" % BM], [("off", t)], ["r%d" % BM])
+        holder[BM] = None
 
-    def repeat(t, k):
-        if t == 0:
-            op("v", lambda: V.tensor_copy(rep[0][:, k:16 * Q:16], vq(0, 0, Q)), vq_keys[0], [("rep", 0, k)])
-        else:
-            op("g", lambda: g.affine_select(rep[t][:, k:16 * Q:16], vq(t, 0, Q), [[0, Q]], ALU.is_ge, 0.0, 0, 0),
-               vq_keys[t], [("rep", t, k)])
+    todo = [(t, k) for t in range(3) for k in range(16)]
+
+    def reps(e, n, upto):
+        for _ in range(n):
+            if todo and todo[0][0] <= upto:
+                t, k = todo.pop(0)
+                o, i = rep[t][:, k:16 * Q:16], vq(t, 0, Q)
+                fn = {"v": lambda: V.tensor_copy(o, i), "a": lambda: S.activation(o, i, ACT.Copy),
+                      "g": lambda: g.affine_select(o, i, [[0, Q]], ALU.is_ge, 0.0, 0, 0)}[e]
+                op(e, fn, vq_keys[t], [("rep", t, k)])
 
     list1(0)
     list2(0)
     list3(0)
-    for k in range(16):
-        repeat(0, k)
+    reps("v", 16, 0)
     list4(0)
     list1(1)
     list2(1)
     list3(1)
+    fill(T.cz[0:32, :], 0.0, "cz")
+    fill(T.one[0:32, :], 1.0, "one")
     fill(T.zmask[:], 1.0, "zmask")
+    fill(T.cz[0:1, 0:128:16], -128.0, "cz")
+    fill(T.cz[0:1, 128:144:2], 0.5, "cz")
     fill(T.zmask[:, 0:CW:16], 0.0, "zmask")
-    todo = [(1, k) for k in range(16)] + [(2, k) for k in range(16)]
+    for m in ("z0e", "z0o", "z0p"):
+        send(m, ["zq0", "zq1"])
+    reps("g", 2, 1)
 
-    def reps(n):
-        for _ in range(n):
-            repeat(*todo.pop(0))
+    outs, slot, aslot = [0], [0], {}
+    first = [sum(GROUPS[:c]) for c in range(len(GROUPS))]
+    group = [c for c, n in enumerate(GROUPS) for _ in range(n)]
 
-    reps(5)
-    deps("g", ["vO0", "vin0"], (), ())
-    g.dma_start(T.w1[:, 0:2048], T.w0[:, 2048:4096]).then_inc(T.sem.cast, 16)
-    wr["cast"] = [("cast", 16)]
+    def place(c):
+        singles = [i for i, n in enumerate(GROUPS) if n == 1]
+        if len(singles) == 2:
+            b, o = (0, 256 * singles.index(c)) if c in singles else (1, 0)
+        else:
+            b, o = first[c] // 2, 256 * (first[c] % 2)
+        return pc[b], ("c", b), o
 
-    outs = [0]
-    nb = [0]
+    def repk(t):
+        return [("rep", t, k) for k in range(16)]
 
-    def layer(t):
-        NB = (1, 2, 1)
-        grp_of_piece = (0, 0, 1, 1, 1, 1, 2, 2)
-        first_piece = (0, 2, 6)
+    def dkeys(p, n=1):
+        return [("d", u) for u in range(2 * p + 4, 2 * (p + n) + 4)]
 
-        def dg(p):
-            o, a = HW * (p % 6), HW * p
-            f = Q * t + a // 16
-            op("v", lambda: V.tensor_tensor(T.dd[:, o:o + HW], vwin[t].indirect(T.off[:, f:f + HW // 16]), rep[t][:, a:a + HW], ALU.subtract),
-               vwin_keys[t] + [("off", t)] + [("rep", t, k) for k in range(16)], [("d", p % 6)])
+    def dg(t, p, n=1):
+        assert not todo or todo[0][0] > t
+        o, a, w = CW + PW * p, PW * p, PW * n
+        src = vwin[t].indirect(T.off[:, Q * t + a // 16:Q * t + (a + w) // 16])
+        keys = vwin_keys[t] + [("off", t)]
+        if p in BY_SCALAR:
+            op("a", lambda: S.activation(T.dd[:, o:o + w], src, ACT.Copy, scale=-1.0), keys, dkeys(p, n))
+            deps("g", repk(t), dkeys(p, n), ())
+            s = "add%d_%d" % (t, p)
+            g.dma_start(T.dd[:, o:o + w], rep[t][:, a:a + w], accum_op=ALU.add).then_inc(T.sem[s], 16)
+            for k in dkeys(p, n):
+                wr[k] = [(s, 16)]
+        else:
+            op("v", lambda: V.tensor_tensor(T.dd[:, o:o + w], src, rep[t][:, a:a + w], ALU.subtract), keys + repk(t), dkeys(p, n))
+        done.update((t, "dg", i) for i in range(p, p + n))
 
-        def ab(p):
-            o, a = HW * (p % 6), HW * (p % 4)
-            op("a", lambda: S.activation(T.aa[:, a:a + HW], T.dd[:, o:o + HW], ACT.Abs), [("d", p % 6)], [("a", p % 4)])
+    def ab(t, p, n=1):
+        need(*[(t, "dg", i) for i in range(p, p + n)])
+        o, a = CW + PW * p, slot[0] % 4
+        assert a + n <= 4 and not set(range(a, a + n)) & set(aslot.values())
+        slot[0] += n
+        for i in range(n):
+            aslot[p + i] = a + i
+        op("a", lambda: S.activation(T.aa[:, PW * a:PW * (a + n)], T.dd[:, o:o + PW * n], ACT.Abs), dkeys(p, n), [("a", a + i) for i in range(n)])
 
-        def smm(p):
-            c = grp_of_piece[p]
-            a, lst = HW * (p % 4), []
-            for i in range(8):
-                n = 8 * (p - first_piece[c]) + i
-                o = 128 * (n % NB[c]) + 8 * (n // NB[c])
-                lst.append((pc[c % 2][:, o:o + 8], T.aa[:, a + 128 * i:a + 128 * i + 128], T.bo[:], True, True))
-            mms(lst, [("a", p % 4), "bo"], [], [("c", c % 2)])
+    def sm(t, p):
+        n, c = aslot.pop(p), group[p // 2]
+        b, key, c0 = place(c)
+        if t and c == 0:
+            need((t - 1, "za", 0))
+        lst = []
+        for i in range(8):
+            j = 8 * (p - 2 * first[c]) + i
+            o = c0 + 128 * (j % GROUPS[c]) + 8 * (j // GROUPS[c])
+            lst.append((b[:, o:o + 8], T.aa[:, PW * n + 128 * i:PW * n + 128 * i + 128], T.bo[:], True, True))
+        mms(lst, [("a", n), "bo"], [], [key])
 
-        def clamp(c):
-            n, b = 128 * NB[c], pc[c % 2]
-            op("a", lambda: S.activation(T.uu[:, 0:n], b[:, 0:n], ACT.Relu, bias=0.25, scale=-1.0 / 128), (), ["u"], [("c", c % 2)])
-            lst = []
-            for i in range(NB[c]):
-                o = b[:, 128 * i:128 * i + 128]
-                lst += [(o, T.uu[:, 128 * i:128 * i + 128], T.shift[:], True, False), (o, T.one[0:1, :], T.cz[0:1, 0:128], False, True)]
-            mms(lst, ["u", "shift", "one", "cz"], [], [("c", c % 2)])
-            op("a", lambda: S.activation(T.wt[:, 0:n], T.uu[:, 0:n], ACT.Exp, bias=-0.25), ["u"], ["w"])
-            lst = []
-            for i in range(NB[c]):
-                o = b[:, n + 16 * i:n + 16 * i + 16]
-                lst += [(o, T.wt[:, 128 * i:128 * i + 128], T.sumb[:], True, False), (o, T.one[0:1, :], T.cz[0:1, 128:144], False, True)]
-            mms(lst, ["w", "sumb"], [], [("c", c % 2)])
+    def relu(t, c):
+        need(*[(t, "sm", p) for p in range(2 * first[c], 2 * first[c] + 2 * GROUPS[c])])
+        b, key, c0 = place(c)
+        n, u = 128 * GROUPS[c], 128 * first[c]
+        op("a", lambda: S.activation(T.uu[:, u:u + n], b[:, c0:c0 + n], ACT.Relu, bias=0.25, scale=-1.0 / 128), (), [("u", c)], [key])
 
-        def ratio(c):
-            n, m, b, h = 128 * NB[c], 144 * NB[c], pc[c % 2], 144 * (c % 2)
-            op("a", lambda: S.activation(b[:, 0:n], b[:, 0:n], ACT.Exp), (), [("x", c % 2)], [("c", c % 2)])
-            op("a", lambda: S.activation(T.hi[:, h:h + m], b[:, 0:m], ACT.Copy), [("x", c % 2)], [("hi", c % 2)], [("c", c % 2)])
+    def turn(c, src, skey, mov, mkey, z0, w, c1):
+        b, key, c0 = place(c)
+        lst = []
+        for i in range(GROUPS[c]):
+            o, u = b[:, c0 + c1 + w * i:c0 + c1 + w * i + w], 128 * (first[c] + i)
+            lst += [(o, src[:, u:u + 128], mov[:], True, False), (o, T.one[0:1, :], T.cz[0:1, z0:z0 + w], False, True)]
+        mms(lst, [(skey, c), mkey, "one", "cz"], [], [key])
 
-        def low(c):
-            m, b, h = 144 * NB[c], pc[c % 2], 144 * (c % 2)
-            op("v", lambda: V.tensor_tensor(T.lo[:, h:h + m], b[:, 0:m], T.hi[:, h:h + m], ALU.subtract),
-               [("hi", c % 2)], [("lo", c % 2)], [("c", c % 2)])
+    def diff(t, c):
+        need((t, "relu", c))
+        turn(c, T.uu, "u", T.shift, "shift", 0, 128, 0)
 
-        held = {}
+    def expw(t, c):
+        need((t, "relu", c))
+        n, u = 128 * GROUPS[c], 128 * first[c]
+        op("a", lambda: S.activation(T.wt[:, u:u + n], T.uu[:, u:u + n], ACT.Exp), [("u", c)], [("w", c)])
 
-        def bc(u):
-            c = grp_of_piece[u // 2]
-            n = nb[0] % 5
-            nb[0] += 1
-            held[u] = n
-            w, h, per = 128 * NB[c], 144 * (c % 2), 4 // NB[c]
-            lst = []
-            for i in range(per):
-                s0 = 128 * (per * (u - 2 * first_piece[c]) + i)
-                o = pr[n][:, w * i:w * i + w]
-                lst.append((o, T.sel[:, s0:s0 + 128], T.hi[:, h:h + w], True, False))
-                lst.append((o, T.sel[:, s0:s0 + 128], T.lo[:, h:h + w], False, True))
-            mms(lst, [("hi", c % 2), ("lo", c % 2), "sel"], [], ["r%d" % n])
+    def sumw(t, c):
+        need((t, "expw", c))
+        turn(c, T.wt, "w", T.sumb, "sumb", 128, 16, 128 * GROUPS[c])
 
-        def scan(u):
-            n = held[u]
-            o, b = 512 * (u % 12), u % 4
-            op("v", lambda: V.tensor_tensor_scan(T.tt[:, 512 * b:512 * b + 512], pr[n][:], T.dd[:, o:o + 512], 0.0, ALU.mult, ALU.add),
-               [("d", (u // 2) % 6)], [("t", b)], ["r%d" % n])
+    def expr(t, c):
+        need((t, "diff", c))
+        b, key, c0 = place(c)
+        n = 128 * GROUPS[c]
+        op("a", lambda: S.activation(b[:, c0:c0 + n], b[:, c0:c0 + n], ACT.Exp), (), [("x", c)], [key])
 
-        def abmm(c):
-            w, h = 16 * NB[c], 144 * (c % 2) + 128 * NB[c]
-            lst = []
-            for i in range(16):
-                o = pc[c % 2][:, w * i:w * i + w]
-                lst.append((o, T.sel[:, 128 * i:128 * i + 128], T.hi[:, h:h + w], True, False))
-                lst.append((o, T.sel[:, 128 * i:128 * i + 128], T.lo[:, h:h + w], False, True))
-            mms(lst, [("hi", c % 2), ("lo", c % 2), "sel"], [], [("c", c % 2)])
+    def high(t, c):
+        need((t, "expr", c), (t, "sumw", c))
+        b, key, c0 = place(c)
+        m, h = 144 * GROUPS[c], 144 * first[c]
+        op("a", lambda: S.activation(T.hi[:, h:h + m], b[:, c0:c0 + m], ACT.Copy), [("x", c)], [("hi", c)], [key])
 
-        def fin(c):
-            bk, o0 = (0, 1, 1, 0)[c], (0, 0, 256, 0)[c]
-            pa, pb = pc[bk][:, o0:o0 + 256:2], pc[bk][:, o0 + 1:o0 + 256:2]
-            op("v", lambda: V.tensor_tensor(pa, vq(t, CQ * c, CQ * c + CQ), pa, ALU.mult), vq_keys[t], [("pa", c)], [("c", bk)])
-            op("v", lambda: V.tensor_tensor(T.tmp[:], T.tt[:, 15:CW:16], pb, ALU.mult), [("t", b) for b in range(4)], ["tmp"], [("c", bk)])
+    def low(t, c):
+        need((t, "high", c))
+        b, key, c0 = place(c)
+        m, h = 144 * GROUPS[c], 144 * first[c]
+        op("v", lambda: V.tensor_tensor(T.lo[:, h:h + m], b[:, c0:c0 + m], T.hi[:, h:h + m], ALU.subtract),
+           [("hi", c)], [("lo", c)], [key])
+
+    def spread(c, out, o0, key, w, h, sels):
+        lst = []
+        for i, s in enumerate(sels):
+            o = out[:, o0 + w * i:o0 + w * i + w]
+            lst.append((o, T.sel[:, 128 * s:128 * s + 128], T.hi[:, h:h + w], True, False))
+            lst.append((o, T.sel[:, 128 * s:128 * s + 128], T.lo[:, h:h + w], False, True))
+        mms(lst, [("hi", c), ("lo", c), "sel"], [], [key])
+
+    def bc(t, u):
+        c = group[u // 4]
+        need((t, "low", c))
+        n, per = take(u, u % 6), 4 // GROUPS[c]
+        s = per * (u - 4 * first[c])
+        spread(c, pair[n // 2], 512 * (n % 2), "r%d" % n, 128 * GROUPS[c], 144 * first[c], range(s, s + per))
+
+    def scan(t, u, n=1):
+        us = range(u, u + n)
+        need(*[(t, "bc", i) for i in us])
+        need(*[(t, "scan", i - 4) for i in us if i >= 4])
+        b, o, w = u % 6, 512 * u, 512 * n
+        op("v", lambda: V.tensor_tensor_scan(T.dd[:, o:o + w], pair[b // 2][:, 512 * (b % 2):512 * (b % 2) + w], T.dd[:, CW + o:CW + o + w],
+                                             0.0, ALU.mult, ALU.add),
+           [("d", i + 4) for i in us], [("d", i) for i in us], ["r%d" % (i % 6) for i in us])
+        for i in us:
+            holder[i % 6] = None
+            done.add((t, "scan", i))
+
+    def abm(t, c):
+        need((t, "low", c))
+        b, key, c0 = place(c)
+        spread(c, b, c0, key, 16 * GROUPS[c], 144 * first[c] + 128 * GROUPS[c], range(16))
+
+    def self_(t, c):
+        need((t, "abm", c))
+        b, key, c0 = place(c)
+        n, q0 = 256 * GROUPS[c], CQ * first[c]
+        pa = b[:, c0:c0 + n:2]
+        op("v", lambda: V.tensor_tensor(pa, vq(t, q0, q0 + n // 2), pa, ALU.mult), vq_keys[t], [("pa", c)], [key])
+
+    def scale(t, f):
+        q0, q1 = FINS[f]
+        c = group[q0 // CQ]
+        us = range(q0 // 32, q1 // 32)
+        need((t, "abm", c), *[(t, "scan", u) for u in us])
+        if f >= 2:
+            need((t, "fin", f - 2))
+        b, key, c0 = place(c)
+        o, m = c0 + 2 * (q0 - CQ * first[c]), 2 * CQ * (f % 2)
+        op("v", lambda: V.tensor_tensor(T.tmp[:, m:m + q1 - q0], T.dd[:, 16 * q0 + 15:16 * q1:16], b[:, o + 1:o + 2 * (q1 - q0):2], ALU.mult),
+           [("d", u) for u in us], [("tmp", f % 2)], [key])
+
+    def fin(t, f):
+        q0, q1 = FINS[f]
+        c = group[q0 // CQ]
+        need((t, "scale", f), (t, "self", c))
+        if f:
+            need((t, "fin", f - 1))
+        if t == 2:
+            need((2, "aside", 0))
+        b, key, c0 = place(c)
+        o0, m = c0 + 2 * (q0 - CQ * first[c]), 2 * CQ * (f % 2)
+        cuts = [q0] + [a for a in range(q0 + 64, q1, 64) if (a // 64 in BY_SCALAR) != (a // 64 - 1 in BY_SCALAR)] + [q1]
+        for a, e in zip(cuts[:-1], cuts[1:]):
             if t < 2:
-                o = 2048 * (t + 1) + own + CQ * c
-                dst = T.w1[:, o:o + CQ]
+                o = 2048 * (t + 1) + own
+                dst = T.w1[:, o + a:o + e]
             else:
-                dst = T.yvs[:, 2 * CQ * c:2 * CQ * (c + 1):2]
-            op("v", lambda: V.tensor_tensor(dst, T.tmp[:], pa, ALU.add), ["tmp", ("pa", c)], [("vnew", t, c)], [("c", bk)])
-            if t < 2:
-                send("v%dc%d" % (t + 1, c), [("vnew", t, c)])
-            else:
-                deps("s", [("vnew", t, c), "yvodd"], (), ())
-                g.sync.dma_start(T.yv[:, 2 * CQ * c:2 * CQ * (c + 1)], T.yvs[:, 2 * CQ * c:2 * CQ * (c + 1)]).then_inc(T.sem.outs, 16)
-                outs[0] += 16
-
-        zp = [0]
-
-        def zg(n):
-            for _ in range(n):
-                p = zp[0]
-                zp[0] += 1
-                op("a", lambda: S.activation(T.zg[:, 512 * p:512 * p + 512],
-                                             T.zw[:, 2048 * t:2048 * t + 4096].indirect(T.off[:, Q * t + 32 * p:Q * t + 32 * p + 32]), ACT.Copy),
-                   zwin_keys[t] + [("off", t)], [("zg", p)])
-
-        def zmax(c):
-            o = CW * (c % 2)
-            op("v", lambda: V.tensor_tensor_scan(T.zs[:, o:o + CW], T.zmask[:], T.zg[:, CW * c:CW * c + CW], 0.0, ALU.mult, ALU.max),
-               ["zmask"] + [("zg", 4 * c + i) for i in range(4)], [("zs", c % 2)])
-            mms([(T.pm[:, CQ * c:CQ * c + CQ], T.mbm[:], T.zs[:, o + 15:o + CW:16], True, True)], [("zs", c % 2), "mats"], [], ["m"])
-
-        def znew(a, b):
-            zi = T.zi[:, a:b]
-            op("v", lambda: V.tensor_copy(zi, T.pm[:, a:b]), (), ["zi"], ["m"])
-            op("v", lambda: V.tensor_scalar(zi, zi, 2, 15, ALU.arith_shift_right, ALU.bitwise_and), ["zi"], ["zi"])
-            if t < 2:
-                o = 2048 * (t + 2) + own
-                op("v", lambda: V.tensor_copy(T.zw[:, o + a:o + b], zi), ["zi"], ["zq%d" % (t + 2)])
-                if b == Q:
-                    send("z%d" % (t + 1), ["zq%d" % (t + 2)])
-            else:
-                op("v", lambda: V.tensor_copy(T.yzs[:, 2 * a:2 * b:2], zi), ["zi"], ["yzeven"])
-                deps("s", ["yzeven", "yzodd"], (), ())
-                g.sync.dma_start(T.yz[:, 2 * a:2 * b], T.yzs[:, 2 * a:2 * b]).then_inc(T.sem.outs, 16)
-                outs[0] += 16
-
-        def early(i):
-            if t == 1:
-                (list1, list2, list3)[i](2)
-            if t == 2 and i == 0:
-                op("a", lambda: S.activation(T.yzs[:, 1:1024:2], zq(3), ACT.Copy), ["zq3"], ["yzodd"])
-                o = 4096 + own
-                op("g", lambda: g.affine_select(T.yvs[:, 1:1024:2], T.w1[:, o:o + Q], [[0, Q]], ALU.is_ge, 0.0, 0, 0),
-                   [("vnew", 1, c) for c in range(NCH)], ["yvodd"])
-
-        nrep = ((5, 3, 2, 1), (8, 3, 2, 0), (0, 0, 0, 0))[t]
-        dg(0); early(0); ab(0); smm(0)
-        dg(1); early(1); ab(1); smm(1)
-        dg(2); early(2); clamp(0); ab(2); ratio(0); smm(2)
-        dg(3); ab(3); smm(3)
-        dg(4); low(0); ab(4); bc(0); bc(1); smm(4); bc(2); bc(3)
-        dg(5); ab(5); smm(5); abmm(0)
-        scan(0); scan(1); scan(2); scan(3)
-        clamp(1); zg(2); ratio(1)
-        reps(nrep[0]); fin(0)
-        dg(6); low(1); zg(1); ab(6); bc(4); bc(5); smm(6); bc(6); bc(7)
-        dg(7); zg(1); ab(7); bc(8); smm(7); abmm(1)
-        scan(4); bc(9); scan(5)
-        zg(1); clamp(2); zg(1); ratio(2)
-        bc(10); scan(6); bc(11); scan(7)
-        reps(nrep[1]); fin(1)
-        scan(8); low(2); bc(12); scan(9); bc(13); scan(10); bc(14); scan(11); bc(15); abmm(2)
-        reps(nrep[2]); fin(2)
-        scan(12); scan(13); scan(14); scan(15); fin(3)
-        reps(nrep[3])
-        zg(10)
+                dst = T.yvs[:, 2 * a:2 * e:2]
+            pa = b[:, o0 + 2 * (a - q0):o0 + 2 * (e - q0):2]
+            op("v", lambda: V.tensor_tensor(dst, pa, T.tmp[:, m + a - q0:m + e - q0], ALU.subtract if a // 64 in BY_SCALAR else ALU.add),
+               [("tmp", f % 2), ("pa", c)], [("vpart", a)], [key])
+        wr[("vnew", t, f)] = [("cv", count["cv"])]
         if t < 2:
-            list4(t + 1)
-        if t == 0:
-            reps(3)
-        zmax(0); zmax(1); zmax(2); znew(0, 3 * CQ); zmax(3); znew(3 * CQ, Q)
+            send("v%dc%d" % (t + 1, f), [("vnew", t, f)])
+        else:
+            deps("s", [("vnew", t, f), "yvodd"], (), ())
+            g.sync.dma_start(T.yv[:, 2 * q0:2 * q1], T.yvs[:, 2 * q0:2 * q1]).then_inc(T.sem.outs, 16)
+            outs[0] += 16
 
-    for t in range(3):
-        layer(t)
+    def zg(t, p, n=1, e="a"):
+        if t:
+            need((t - 1, "zc", len(ZHALF) - 1))
+        o = T.zg[:, PW * p:PW * (p + n)]
+        src = T.zw[:, 2048 * t:2048 * t + 4096].indirect(T.off[:, Q * t + 64 * p:Q * t + 64 * (p + n)])
+        fn = {"a": lambda: S.activation(o, src, ACT.Copy), "v": lambda: V.tensor_copy(o, src)}[e]
+        op(e, fn, zwin_keys[t] + [("off", t)], [("zg", i) for i in range(p, p + n)])
+        done.update((t, "zg", i) for i in range(p, p + n))
+
+    zbank = [("c", 0), "r5"]
+
+    def zout(a, n):
+        return T.pr2[:, 256 + a:256 + a + n] if a >= 256 else T.pc0[:, a:a + n]
+
+    def zmax(t, c):
+        need((t, "zg", 2 * c), (t, "zg", 2 * c + 1))
+        if c < 2:
+            need((t, "fin", 0))
+        elif holder.get(5) != "z":
+            assert (t, "zmax", 5 - c) not in done
+            take("z", 5)
+        o = CW * (c % 2)
+        op("v", lambda: V.tensor_tensor_scan(T.zs[:, o:o + CW], T.zmask[:], T.zg[:, CW * c:CW * c + CW], 0.0, ALU.mult, ALU.max),
+           ["zmask", ("zg", 2 * c), ("zg", 2 * c + 1)], [("zs", c % 2)])
+        mms([(zout(CQ * c, CQ), T.mbm[:], T.zs[:, o + 15:o + CW:16], True, True)], [("zs", c % 2), "mats"], [], [zbank[c // 2]])
+
+    def za(t, h):
+        a, b = ZHALF[h]
+        need(*[(t, "zmax", c) for c in range(a // CQ, b // CQ)])
+        op("v", lambda: V.tensor_copy(T.zi[:, a:b], zout(a, b - a)), (), [("zi", h)], [zbank[h]])
+        if h:
+            holder[5] = None
+
+    def zb(t, h):
+        a, b = ZHALF[h]
+        need((t, "za", h))
+        op("v", lambda: V.tensor_scalar(T.zi[:, a:b], T.zi[:, a:b], 2, 15, ALU.arith_shift_right, ALU.bitwise_and), [("zi", h)], [("zi", h)])
+
+    def zc(t, h):
+        a, b = ZHALF[h]
+        need((t, "zb", h))
+        if h:
+            need((t, "zc", h - 1))
+        if t < 2:
+            o = 2048 * (t + 2) + own
+            op("v", lambda: V.tensor_copy(T.zw[:, o + a:o + b], T.zi[:, a:b]), [("zi", h)], [("zpart", h)])
+            send("z%dc%d" % (t + 1, h), [("zpart", h)])
+            if b == Q:
+                wr["zq%d" % (t + 2)] = [("cv", count["cv"])]
+                if t == 1:
+                    op("g", lambda: g.affine_select(T.yzs[:, 1:1024:2], zq(3), [[0, Q]], ALU.is_ge, 0.0, 0, 0), ["zq3"], ["yzodd"])
+        else:
+            op("v", lambda: V.tensor_copy(T.yzs[:, 2 * a:2 * b:2], T.zi[:, a:b]), [("zi", h)], [("zpart", h)])
+            deps("s", [("zpart", h), "yzodd"], (), ())
+            g.sync.dma_start(T.yz[:, 2 * a:2 * b], T.yzs[:, 2 * a:2 * b]).then_inc(T.sem.outs, 16)
+            outs[0] += 16
+
+    def aside(t, i):
+        if t == 0:
+            deps("g", ["vO0", "vin0"], (), ())
+            g.dma_start(T.w1[:, 0:2048], T.w0[:, 2048:4096]).then_inc(T.sem.cast, 16)
+            wr["cast"] = [("cast", 16)]
+        if t == 2:
+            o = 4096 + own
+            op("g", lambda: g.affine_select(T.yvs[:, 1:1024:2], T.w1[:, o:o + Q], [[0, Q]], ALU.is_ge, 0.0, 0, 0), vnew[1], ["yvodd"])
+
+    def lst(t, i):
+        if t == 0 and i == 0:
+            list4(1)
+        if t == 1 and i:
+            need((0, "zc", len(ZHALF) - 1))
+            if i > 1:
+                need((t, "list", i - 1))
+            (list1, list2, list3, list4)[i - 1](2)
+
+    steps = {"dg": dg, "DG": lambda t, p: dg(t, p, 2), "ab": ab, "AB": lambda t, p: ab(t, p, 2), "sm": sm, "relu": relu, "diff": diff,
+             "expw": expw, "sumw": sumw, "expr": expr, "high": high, "low": low, "bc": bc, "scan": scan,
+             "SCAN": lambda t, p: scan(t, 2 * p, 2), "abm": abm, "self": self_, "scale": scale, "fin": fin, "zg": zg,
+             "ZG": lambda t, c: zg(t, 2 * c, 2), "zv": lambda t, p: zg(t, p, 1, "v"), "zmax": zmax, "za": za, "zb": zb, "zc": zc,
+             "aside": aside, "list": lst, "rep": lambda t, i: reps("g", 2, t + 1)}
+    for t in range(4):
+        for word in ORDER.split():
+            late = word.startswith("-")
+            name = word.strip("-0123456789")
+            tt, i = t - late, int(word[late + len(name):])
+            if 0 <= tt < 3:
+                steps[name](tt, i)
+                done.add((tt, name, i))
 
     g.wait_ge(T.sem.sent, sent[0])
     wait("s", [(s, v) for s, v in count.items()])

import math
from concourse.bass import DstId, RemoteDMATransfer
from concourse.mybir import AluOpType, ActivationFunctionType

ALU = AluOpType
ACT = ActivationFunctionType
Q, CQ = 512, 128
CW = 16 * CQ
PW = CW // 2
GROUPS = (1, 2, 1)
FINS = ((0, 128), (128, 384), (384, 512))
BY_SCALAR = (4, 5)
ZHALF = ((0, 256), (256, 512))
ORDER = """dg4 dg0 dg5 dg1 ab0 rep0 rep1 sm0 dg2 ab1 dg3 ab2 sm1 relu0 sm2 expw0 -za1 ab3 -zb1 -zc1 list0 diff0 sumw0 expr0 sm3 high0
ab4 low0 dg6 rep2 ab5 dg7 abm0 bc0 sm4 ab6 sm5 rep3 aside0 relu1 bc1 expw1 bc2 diff1 bc3 sumw1 SCAN0 ab7 SCAN1 expr1 rep4 high1
sm6 sm7 low1 self0 zg0 scale0 bc4 bc5 fin0 bc6 SCAN2 rep5 bc7 relu2 expw2 sumw2 bc8 SCAN3 bc9 bc10 bc11 SCAN4 zg1 diff2 expr2
abm1 high2 SCAN5 rep6 low2 self1 scale1 bc12 bc13 fin1 SCAN6 bc14 bc15 abm2 zg2 zg3 zg4 SCAN7 rep7 list1 self2 scale2 fin2
zmax0 zmax1 zg5 list2 list3 zv7 zg6 za0 zmax2 zb0 list4 zmax3 zc0"""

SCRATCH = {
    "vin": ("sbuf", [128, 1024], "bfloat16"),
    "zin": ("sbuf", [128, 1024], "bfloat16"),
    "w0": ("sbuf", [128, 4096], "bfloat16"),
    "w1": ("sbuf", [128, 6144], "float32"),
    "zw": ("sbuf", [128, 8192], "bfloat16"),
    "may": ("sbuf", [128, 128], "bfloat16"),
    "mxx": ("sbuf", [128, 128], "bfloat16"),
    "mbm": ("sbuf", [128, 128], "bfloat16"),
    "ident": ("sbuf", [128, 128], "bfloat16"),
    "idp": ("sbuf", [128, 128], "bfloat16"),
    "idm": ("sbuf", [128, 128], "bfloat16"),
    "ypos": ("sbuf", [128, Q], "bfloat16"),
    "xpos": ("sbuf", [128, Q], "bfloat16"),
    "fy": ("sbuf", [128, Q], "bfloat16"),
    "fx": ("sbuf", [128, Q], "bfloat16"),
    "y16": ("sbuf", [128, Q], "bfloat16"),
    "x16": ("sbuf", [128, Q], "bfloat16"),
    "x8": ("sbuf", [128, Q], "bfloat16"),
    "off": ("sbuf", [128, 3 * Q], "uint16"),
    "rep0": ("sbuf", [128, 16 * Q], "bfloat16"),
    "rep1": ("sbuf", [128, 16 * Q], "bfloat16"),
    "rep2": ("sbuf", [128, 16 * Q], "float32"),
    "dd": ("sbuf", [128, 5 * CW], "float32"),
    "aa": ("sbuf", [128, 4 * PW], "float32"),
    "tmp": ("sbuf", [128, 4 * CQ], "float32"),
    "uu": ("sbuf", [128, Q], "float32"),
    "wt": ("sbuf", [128, Q], "float32"),
    "hi": ("sbuf", [128, 4 * 144], "bfloat16"),
    "lo": ("sbuf", [128, 4 * 144], "float16"),
    "sel": ("sbuf", [128, 2048], "bfloat16"),
    "bo": ("sbuf", [128, 8], "float32"),
    "shift": ("sbuf", [128, 128], "float32"),
    "sumb": ("sbuf", [128, 16], "float32"),
    "cz": ("sbuf", [128, 144], "bfloat16"),
    "one": ("sbuf", [128, 128], "bfloat16"),
    "zg": ("sbuf", [128, 16 * Q], "bfloat16"),
    "zs": ("sbuf", [128, 2 * CW], "bfloat16"),
    "zmask": ("sbuf", [128, CW], "bfloat16"),
    "zi": ("sbuf", [128, Q], "int32"),
    "yvs": ("sbuf", [128, 1024], "float32"),
    "yzs": ("sbuf", [128, 1024], "float32"),
    "pc0": ("psum", [128, 512], "float32"),
    "pc1": ("psum", [128, 512], "float32"),
    "pr0": ("psum", [128, 1024], "float32"),
    "pr1": ("psum", [128, 1024], "float32"),
    "pr2": ("psum", [128, 1024], "float32"),
}
MSGS = (["v0e", "v0o", "v0p", "z0e", "z0o", "z0p"] + ["v1c%d" % c for c in range(len(FINS))] + ["z1c0", "z1c1"]
        + ["v2c%d" % c for c in range(len(FINS))] + ["z2c0", "z2c1"])
SEMAPHORES = (["cv", "ca", "cp", "cg", "ldv", "ldz", "ldm", "cast", "outs", "sent"]
              + ["ar_" + s for s in ("v0", "z0", "v1", "z1", "v2", "z2")] + ["m_" + m for m in MSGS]
              + ["add%d_%d" % (t, p) for t in range(3) for p in range(8)])


def routes(T, topo):
    cores = list(T.cores)
    calls, arrivals = {}, {}

    def add(src, msg, call):
        calls.setdefault(src, {}).setdefault(msg, []).append(call)
        for (_b, _c, _w, dst, eng, sem) in call:
            arrivals[(dst, sem)] = arrivals.get((dst, sem), 0) + len(eng)

    world = range(max(topo.cores_of(max(cores))) + 1 + len(topo.cores_of(cores[0])))
    for r, me in enumerate(cores):
        others = [c for c in cores if c != me]
        peer = [c for c in others if topo.may_write(me, c)][0]
        rest = [c for c in others if c != peer]
        a = [c for c in rest if topo.host(c) == topo.host(me)][0]
        b = [c for c in rest if c != a][0]
        relays = [c for c in topo.cores_of(me) if c != me and topo.may_write(c, a) and topo.may_write(c, b)]
        near = [c for c in relays if topo.die(c) == topo.die(me)]
        far = [c for c in relays if topo.die(c) != topo.die(me)]
        mate = [c for c in world if topo.mates(c, a) and topo.may_write(c, a) and topo.may_write(me, c)]
        mate = [[c for c in mate if topo.die(c) == d][0] for d in sorted(set(topo.die(c) for c in mate))]
        eoff = topo.engines(me, peer)
        erest = [e for e in topo.engines(me, relays[0]) if e not in eoff]
        h = len(eoff) // 2
        for n, msg in enumerate(MSGS):
            fin, hop = "ar_" + msg[:2], "m_" + msg
            if msg[1] == "0":
                buf = "w0" if msg[0] == "v" else "zw"
                ce, co = Q * r, 2048 + Q * r
                if msg[2] == "p":
                    add(me, msg, [(buf, ce, Q, peer, eoff[:h], fin), (buf, co, Q, peer, eoff[h:], fin)])
                else:
                    i = "eo".index(msg[2])
                    col, mine = (ce, co)[i], (far[0], near[0])[i]
                    add(me, msg, [(buf, col, Q, mate[i], eoff, hop), (buf, col, Q, mine, erest, hop)])
                    add(mate[i], msg, [(buf, col, Q, a, topo.engines(mate[i], a), fin)])
                    add(mine, msg, [(buf, col, Q, b, topo.engines(mine, b), fin)])
            else:
                t = int(msg[1])
                if msg[0] == "v":
                    q0, q1 = FINS[int(msg[3])]
                    buf, col, w = "w1", 2048 * t + Q * r + q0, q1 - q0
                else:
                    q0, q1 = ZHALF[int(msg[3])]
                    buf, col, w = "zw", 2048 * (t + 1) + Q * r + q0, q1 - q0
                f0, n0 = far[n % 2], near[n % 2]
                if q1 == Q:
                    add(me, msg, [(buf, col, w, n0, eoff, hop), (buf, col, w, f0, erest, hop)])
                    add(me, msg, [(buf, col, w, peer, eoff, fin)])
                else:
                    add(me, msg, [(buf, col, w, peer, eoff, fin), (buf, col, w, n0, erest[:h], hop), (buf, col, w, f0, erest[h:], hop)])
                add(n0, msg, [(buf, col, w, a, topo.engines(n0, a), fin)])
                add(f0, msg, [(buf, col, w, b, topo.engines(f0, b), fin)])
    return calls, arrivals


def issue(g, core, T, topo, call):
    trs, total = [], 0
    for (buf, col, w, dst, eng, sem) in call:
        rid, pid = topo.addr(dst, core)
        m = 0
        for e in eng:
            m |= 1 << e
        ap = T[buf][:, col:col + w]
        trs.append(RemoteDMATransfer(dst_ids=[DstId(rid=rid, pnc=pid)], dma_engine_mask=m, remote_sem=T.sem[sem], src=ap, dst=ap))
        total += len(eng)
    g.remote_dma_fused(trs, local_sem=T.sem.sent)
    return total


def rank_program(g, core, T, topo):
    calls, arrivals = routes(T, topo)
    rank = T.rank_of(core)
    if rank is None:
        total = 0
        for msg in MSGS:
            for call in calls.get(core, {}).get(msg, []):
                g.wait_ge(T.sem["m_" + msg], arrivals[(core, "m_" + msg)])
                total += issue(g, core, T, topo, call)
        if total:
            g.wait_ge(T.sem.sent, total)
        return

    qs = {"v": g.vector, "a": g.scalar, "p": g.tensor, "g": g, "s": g.sync}
    semof = {"v": "cv", "a": "ca", "p": "cp", "g": "cg"}
    count = {"cv": 0, "ca": 0, "cp": 0, "cg": 0}
    waited = {e: {} for e in qs}
    wr, rd, bank = {}, {}, {}
    sent = [0]

    def wait(e, toks):
        most = {}
        for s, v in toks:
            if v > waited[e].get(s, 0) and v > most.get(s, 0):
                most[s] = v
        for s, v in most.items():
            qs[e].wait_ge(T.sem[s], v)
            waited[e][s] = v

    def deps(e, reads, writes, banks):
        toks = []
        for k in reads:
            toks += wr.get(k, [])
        for k in writes:
            toks += wr.get(k, []) + rd.get(k, [])
        for b in banks:
            toks += [tk for (e2, tk) in bank.get(b, {}).items() if e2 != e]
        if e == "p":
            toks = [tk for tk in toks if tk[0] != "cp"]
        wait(e, toks)

    def op(e, fn, reads=(), writes=(), banks=()):
        deps(e, reads, writes, banks)
        s = semof[e]
        count[s] += 1
        fn().then_inc(T.sem[s], 1)
        tok = (s, count[s])
        for k in reads:
            rd.setdefault(k, []).append(tok)
        for k in writes:
            wr[k] = [tok]
            rd[k] = []
        for b in banks:
            bank.setdefault(b, {})[e] = tok

    def mms(lst, reads=(), writes=(), banks=()):
        def fn():
            for (o, l, r_, st, sp) in lst[:-1]:
                g.tensor.matmul(o, l, r_, st, sp)
            o, l, r_, st, sp = lst[-1]
            return g.tensor.matmul(o, l, r_, st, sp)
        op("p", fn, reads, writes, banks)

    def send(msg, reads):
        deps("g", reads, (), ())
        for call in calls[core][msg]:
            sent[0] += issue(g, core, T, topo, call)

    V, S = g.vector, g.scalar
    own = Q * rank
    pc = [T.pc0, T.pc1]
    pair = [T.pr0, T.pr1, T.pr2]
    pr = [b[:, o:o + 512] for b in pair for o in (0, 512)]
    rep = [T.rep0, T.rep1, T.rep2]
    vnew = [[("vnew", t, c) for c in range(len(FINS))] for t in range(3)]
    vwin = [T.w0[:, 0:4096], T.w1[:, 0:4096], T.w1[:, 2048:6144]]
    vwin_keys = [["vE0", "vO0", "vin0"], ["cast", "vin1"] + vnew[0], ["vin1", "vin2"] + vnew[0] + vnew[1]]
    zwin_keys = [["zq0", "zq1", "zin0"], ["zq1", "zq2", "zin0", "zin1"], ["zq2", "zq3", "zin1", "zin2"]]
    vq_keys = [["vE0"], ["vO0"], vnew[0]]
    for kind in "vz":
        for i in range(3):
            s = "ar_%s%d" % (kind, i)
            wr["%sin%d" % (kind, i)] = [(s, arrivals[(core, s)])]

    def vq(t, a, b):
        if t == 2:
            return T.w1[:, 2048 + own + a:2048 + own + b]
        return T.w0[:, 2048 * t + own + a:2048 * t + own + b]

    g.sync.dma_start(T.vin[:], T.v0[:]).then_inc(T.sem.ldv, 16)
    g.sync.dma_start(T.zin[:], T.z0[:]).then_inc(T.sem.ldz, 16)
    g.sync.dma_start(T.may[:], T.ay[:]).then_inc(T.sem.ldm, 16)
    g.sync.dma_start(T.mxx[:], T.ax[:]).then_inc(T.sem.ldm, 16)
    g.sync.dma_start(T.mbm[:], T.bm[:]).then_inc(T.sem.ldm, 16)
    wr["vin"], wr["zin"], wr["mats"] = [("ldv", 16)], [("ldz", 16)], [("ldm", 48)]

    def fill(ap, val, key):
        op("v", lambda: V.memset(ap, val), (), [key])

    def select(ap, pattern, cmp, fillv, base, cm, key):
        op("g", lambda: g.affine_select(ap, ap, pattern, cmp, fillv, base, cm), [key], [key])

    fill(T.ident[:], 1.0, "ident")
    op("g", lambda: g.iota(T.ypos[:], [[8, 32], [0, 16]], 256 * rank, 0, allow_small_or_imprecise_dtypes=True), (), ["ypos"])
    select(T.ident[:], [[-1, 128]], ALU.is_equal, 0.0, 0, 1, "ident")
    fill(T.bo[:], 1.0, "bo")
    fill(T.shift[:], 1.0, "shift")
    fill(T.sumb[:], -0.25 - math.log(64.0), "sumb")
    op("a", lambda: S.activation(T.sumb[:], T.sumb[:], ACT.Exp), ["sumb"], ["sumb"])
    for j in range(16):
        fill(T.xpos[:, j:Q:16], 16.0 * j, ("xpos", j))

    op("v", lambda: V.tensor_copy(T.w0[:, own:own + Q], T.vin[:, 0:1024:2]), ["vin"], ["vE0"])
    send("v0e", ["vE0"])
    op("v", lambda: V.tensor_copy(T.w0[:, 2048 + own:2048 + own + Q], T.vin[:, 1:1024:2]), ["vin"], ["vO0"])
    send("v0o", ["vO0"])
    send("v0p", ["vE0", "vO0"])
    op("v", lambda: V.tensor_copy(T.zw[:, own:own + Q], T.zin[:, 0:1024:2]), ["zin"], ["zq0"])
    op("v", lambda: V.tensor_copy(T.zw[:, 2048 + own:2048 + own + Q], T.zin[:, 1:1024:2]), ["zin"], ["zq1"])
    op("v", lambda: V.tensor_scalar(T.idp[:], T.ident[:], 4096.0, None, ALU.mult), ["ident"], ["idp"])
    op("v", lambda: V.tensor_scalar(T.idm[:], T.ident[:], -4096.0, None, ALU.mult), ["ident"], ["idm"])
    fill(T.sel[:], 1.0, "sel")
    select(T.bo[:], [[-16, 8]], ALU.is_ge, 0.0, 0, 1, "bo")
    select(T.shift[:], [[-1, 128]], ALU.is_equal, 0.0, 1, 1, "shift")
    select(T.sumb[:], [[-16, 8], [-15, 2]], ALU.is_ge, 0.0, 0, 1, "sumb")
    select(T.bo[:], [[16, 8]], ALU.is_ge, 0.0, 15, -1, "bo")
    select(T.shift[:], [[-1, 128]], ALU.not_equal, -1.0, 0, 1, "shift")
    select(T.sumb[:], [[16, 8], [0, 2]], ALU.is_ge, 0.0, 15, -1, "sumb")
    select(T.shift[:], [[0, 8], [1, 16]], ALU.is_gt, 0.0, 0, 0, "shift")
    select(T.sel[:], [[-1, 128], [0, 16]], ALU.is_equal, 0.0, 0, 1, "sel")

    xk = [("xpos", j) for j in range(16)]
    holder, done = {}, set()

    def need(*names):
        for n in names:
            assert n in done, n

    def take(who, n):
        assert holder.get(n) is None
        holder[n] = who
        return n

    def zq(t):
        return T.zw[:, 2048 * t + own:2048 * t + own + Q]

    def ident_act(out, n, scale, bias, okey):
        b = "r%d" % n
        op("a", lambda: S.activation(out, pr[n], ACT.Identity, bias=float(bias), scale=float(scale)), [b], [okey], [b])

    BY, BX, BM = 0, 2, 4

    def list1(t):
        k = ["mats", "ident", "zq%d" % t]
        take("y", BY)
        take("x", BX)
        for n, m, pos, pk in ((BY, T.may, T.ypos, ["ypos"]), (BX, T.mxx, T.xpos, xk)):
            mms([(pr[n], m[:], zq(t), True, False), (pr[n], T.ident[:], pos[:], False, True)], k + pk, ["r%d" % n], ["r%d" % n])
        ident_act(T.fy[:], BY, -1, -196096.5, "fy")
        ident_act(T.fx[:], BX, -1, -49024.5 - 8 * (t % 2), "fx")
        for n, m, pos, f, fk in ((BY, T.may, T.ypos, T.fy, "fy"), (BX, T.mxx, T.xpos, T.fx, "fx")):
            mms([(pr[n], m[:], zq(t), True, False), (pr[n], T.ident[:], pos[:], False, False),
                 (pr[n], T.ident[:], f[:], False, True)], [fk], ["r%d" % n], ["r%d" % n])

    def list2(t):
        ident_act(T.y16[:], BY, 2, 393216 + 2057, "y16")
        holder[BY] = None

    def list3(t):
        s = 1 - 2 * (t % 2)
        c = 8 * (t % 2) + 49152
        ident_act(T.x16[:], BX, 1.0 / 16, c / 16 - 15.0 / 32 + 192, "x16")
        ident_act(T.x8[:], BX, 256 * s, s * (256 * c + 392320), "x8")
        holder[BX] = None
        big = T.idm if s > 0 else T.idp
        pm = pr[take("m", BM)]
        mms([(pm, T.ident[:], T.y16[:], True, False), (pm, T.ident[:], T.x16[:], False, False),
             (pm, big[:], T.x16[:], False, False), (pm, T.ident[:], T.x8[:], False, True)],
            ["y16", "x16", "x8", "idp", "idm"], ["r%d" % BM], ["r%d" % BM])

    def list4(t):
        s = 1 - 2 * (t % 2)
        c = -2064 - 192 * (1 - 4096 * s) - 2048 * 192 * s + (2048 if s < 0 else 0)
        op("v", lambda: V.tensor_scalar(T.off[:, Q * t:Q * t + Q], pr[BM], float(c), None, ALU.add), ["r%d" % BM], [("off", t)], ["r%d" % BM])
        holder[BM] = None

    todo = [(t, k) for t in range(3) for k in range(16)]

    def reps(e, n, upto):
        for _ in range(n):
            if todo and todo[0][0] <= upto:
                t, k = todo.pop(0)
                o, i = rep[t][:, k:16 * Q:16], vq(t, 0, Q)
                fn = {"v": lambda: V.tensor_copy(o, i), "a": lambda: S.activation(o, i, ACT.Copy),
                      "g": lambda: g.affine_select(o, i, [[0, Q]], ALU.is_ge, 0.0, 0, 0)}[e]
                op(e, fn, vq_keys[t], [("rep", t, k)])

    list1(0)
    list2(0)
    list3(0)
    reps("v", 16, 0)
    list4(0)
    list1(1)
    list2(1)
    list3(1)
    fill(T.cz[0:32, :], 0.0, "cz")
    fill(T.one[0:32, :], 1.0, "one")
    fill(T.zmask[:], 1.0, "zmask")
    fill(T.cz[0:1, 0:128:16], -128.0, "cz")
    fill(T.cz[0:1, 128:144:2], 0.5, "cz")
    fill(T.zmask[:, 0:CW:16], 0.0, "zmask")
    for m in ("z0e", "z0o", "z0p"):
        send(m, ["zq0", "zq1"])
    reps("g", 2, 1)

    outs, slot, aslot = [0], [0], {}
    first = [sum(GROUPS[:c]) for c in range(len(GROUPS))]
    group = [c for c, n in enumerate(GROUPS) for _ in range(n)]

    def place(c):
        singles = [i for i, n in enumerate(GROUPS) if n == 1]
        if len(singles) == 2:
            b, o = (0, 256 * singles.index(c)) if c in singles else (1, 0)
        else:
            b, o = first[c] // 2, 256 * (first[c] % 2)
        return pc[b], ("c", b), o

    def repk(t):
        return [("rep", t, k) for k in range(16)]

    def dkeys(p, n=1):
        return [("d", u) for u in range(2 * p + 4, 2 * (p + n) + 4)]

    def dg(t, p, n=1):
        assert not todo or todo[0][0] > t
        o, a, w = CW + PW * p, PW * p, PW * n
        src = vwin[t].indirect(T.off[:, Q * t + a // 16:Q * t + (a + w) // 16])
        keys = vwin_keys[t] + [("off", t)]
        if p in BY_SCALAR:
            op("a", lambda: S.activation(T.dd[:, o:o + w], src, ACT.Copy, scale=-1.0), keys, dkeys(p, n))
            deps("g", repk(t), dkeys(p, n), ())
            s = "add%d_%d" % (t, p)
            g.dma_start(T.dd[:, o:o + w], rep[t][:, a:a + w], accum_op=ALU.add).then_inc(T.sem[s], 16)
            for k in dkeys(p, n):
                wr[k] = [(s, 16)]
        else:
            op("v", lambda: V.tensor_tensor(T.dd[:, o:o + w], src, rep[t][:, a:a + w], ALU.subtract), keys + repk(t), dkeys(p, n))
        done.update((t, "dg", i) for i in range(p, p + n))

    def ab(t, p, n=1):
        need(*[(t, "dg", i) for i in range(p, p + n)])
        o, a = CW + PW * p, slot[0] % 4
        assert a + n <= 4 and not set(range(a, a + n)) & set(aslot.values())
        slot[0] += n
        for i in range(n):
            aslot[p + i] = a + i
        op("a", lambda: S.activation(T.aa[:, PW * a:PW * (a + n)], T.dd[:, o:o + PW * n], ACT.Abs), dkeys(p, n), [("a", a + i) for i in range(n)])

    def sm(t, p):
        n, c = aslot.pop(p), group[p // 2]
        b, key, c0 = place(c)
        if t and c == 0:
            need((t - 1, "za", 0))
        lst = []
        for i in range(8):
            j = 8 * (p - 2 * first[c]) + i
            o = c0 + 128 * (j % GROUPS[c]) + 8 * (j // GROUPS[c])
            lst.append((b[:, o:o + 8], T.aa[:, PW * n + 128 * i:PW * n + 128 * i + 128], T.bo[:], True, True))
        mms(lst, [("a", n), "bo"], [], [key])

    def relu(t, c):
        need(*[(t, "sm", p) for p in range(2 * first[c], 2 * first[c] + 2 * GROUPS[c])])
        b, key, c0 = place(c)
        n, u = 128 * GROUPS[c], 128 * first[c]
        op("a", lambda: S.activation(T.uu[:, u:u + n], b[:, c0:c0 + n], ACT.Relu, bias=0.25, scale=-1.0 / 128), (), [("u", c)], [key])

    def turn(c, src, skey, mov, mkey, z0, w, c1):
        b, key, c0 = place(c)
        lst = []
        for i in range(GROUPS[c]):
            o, u = b[:, c0 + c1 + w * i:c0 + c1 + w * i + w], 128 * (first[c] + i)
            lst += [(o, src[:, u:u + 128], mov[:], True, False), (o, T.one[0:1, :], T.cz[0:1, z0:z0 + w], False, True)]
        mms(lst, [(skey, c), mkey, "one", "cz"], [], [key])

    def diff(t, c):
        need((t, "relu", c))
        turn(c, T.uu, "u", T.shift, "shift", 0, 128, 0)

    def expw(t, c):
        need((t, "relu", c))
        n, u = 128 * GROUPS[c], 128 * first[c]
        op("a", lambda: S.activation(T.wt[:, u:u + n], T.uu[:, u:u + n], ACT.Exp), [("u", c)], [("w", c)])

    def sumw(t, c):
        need((t, "expw", c))
        turn(c, T.wt, "w", T.sumb, "sumb", 128, 16, 128 * GROUPS[c])

    def expr(t, c):
        need((t, "diff", c))
        b, key, c0 = place(c)
        n = 128 * GROUPS[c]
        op("a", lambda: S.activation(b[:, c0:c0 + n], b[:, c0:c0 + n], ACT.Exp), (), [("x", c)], [key])

    def high(t, c):
        need((t, "expr", c), (t, "sumw", c))
        b, key, c0 = place(c)
        m, h = 144 * GROUPS[c], 144 * first[c]
        op("a", lambda: S.activation(T.hi[:, h:h + m], b[:, c0:c0 + m], ACT.Copy), [("x", c)], [("hi", c)], [key])

    def low(t, c):
        need((t, "high", c))
        b, key, c0 = place(c)
        m, h = 144 * GROUPS[c], 144 * first[c]
        op("v", lambda: V.tensor_tensor(T.lo[:, h:h + m], b[:, c0:c0 + m], T.hi[:, h:h + m], ALU.subtract),
           [("hi", c)], [("lo", c)], [key])

    def spread(c, out, o0, key, w, h, sels):
        lst = []
        for i, s in enumerate(sels):
            o = out[:, o0 + w * i:o0 + w * i + w]
            lst.append((o, T.sel[:, 128 * s:128 * s + 128], T.hi[:, h:h + w], True, False))
            lst.append((o, T.sel[:, 128 * s:128 * s + 128], T.lo[:, h:h + w], False, True))
        mms(lst, [("hi", c), ("lo", c), "sel"], [], [key])

    def bc(t, u):
        c = group[u // 4]
        need((t, "low", c))
        n, per = take(u, u % 6), 4 // GROUPS[c]
        s = per * (u - 4 * first[c])
        spread(c, pair[n // 2], 512 * (n % 2), "r%d" % n, 128 * GROUPS[c], 144 * first[c], range(s, s + per))

    def scan(t, u, n=1):
        us = range(u, u + n)
        need(*[(t, "bc", i) for i in us])
        need(*[(t, "scan", i - 4) for i in us if i >= 4])
        b, o, w = u % 6, 512 * u, 512 * n
        op("v", lambda: V.tensor_tensor_scan(T.dd[:, o:o + w], pair[b // 2][:, 512 * (b % 2):512 * (b % 2) + w], T.dd[:, CW + o:CW + o + w],
                                             0.0, ALU.mult, ALU.add),
           [("d", i + 4) for i in us], [("d", i) for i in us], ["r%d" % (i % 6) for i in us])
        for i in us:
            holder[i % 6] = None
            done.add((t, "scan", i))

    def abm(t, c):
        need((t, "low", c))
        b, key, c0 = place(c)
        spread(c, b, c0, key, 16 * GROUPS[c], 144 * first[c] + 128 * GROUPS[c], range(16))

    def self_(t, c):
        need((t, "abm", c))
        b, key, c0 = place(c)
        n, q0 = 256 * GROUPS[c], CQ * first[c]
        pa = b[:, c0:c0 + n:2]
        op("v", lambda: V.tensor_tensor(pa, vq(t, q0, q0 + n // 2), pa, ALU.mult), vq_keys[t], [("pa", c)], [key])

    def scale(t, f):
        q0, q1 = FINS[f]
        c = group[q0 // CQ]
        us = range(q0 // 32, q1 // 32)
        need((t, "abm", c), *[(t, "scan", u) for u in us])
        if f >= 2:
            need((t, "fin", f - 2))
        b, key, c0 = place(c)
        o, m = c0 + 2 * (q0 - CQ * first[c]), 2 * CQ * (f % 2)
        op("v", lambda: V.tensor_tensor(T.tmp[:, m:m + q1 - q0], T.dd[:, 16 * q0 + 15:16 * q1:16], b[:, o + 1:o + 2 * (q1 - q0):2], ALU.mult),
           [("d", u) for u in us], [("tmp", f % 2)], [key])

    def fin(t, f):
        q0, q1 = FINS[f]
        c = group[q0 // CQ]
        need((t, "scale", f), (t, "self", c))
        if f:
            need((t, "fin", f - 1))
        if t == 2:
            need((2, "aside", 0))
        b, key, c0 = place(c)
        o0, m = c0 + 2 * (q0 - CQ * first[c]), 2 * CQ * (f % 2)
        cuts = [q0] + [a for a in range(q0 + 64, q1, 64) if (a // 64 in BY_SCALAR) != (a // 64 - 1 in BY_SCALAR)] + [q1]
        for a, e in zip(cuts[:-1], cuts[1:]):
            if t < 2:
                o = 2048 * (t + 1) + own
                dst = T.w1[:, o + a:o + e]
            else:
                dst = T.yvs[:, 2 * a:2 * e:2]
            pa = b[:, o0 + 2 * (a - q0):o0 + 2 * (e - q0):2]
            op("v", lambda: V.tensor_tensor(dst, pa, T.tmp[:, m + a - q0:m + e - q0], ALU.subtract if a // 64 in BY_SCALAR else ALU.add),
               [("tmp", f % 2), ("pa", c)], [("vpart", a)], [key])
        wr[("vnew", t, f)] = [("cv", count["cv"])]
        if t < 2:
            send("v%dc%d" % (t + 1, f), [("vnew", t, f)])
        else:
            deps("s", [("vnew", t, f), "yvodd"], (), ())
            g.sync.dma_start(T.yv[:, 2 * q0:2 * q1], T.yvs[:, 2 * q0:2 * q1]).then_inc(T.sem.outs, 16)
            outs[0] += 16

    def zg(t, p, n=1, e="a"):
        if t:
            need((t - 1, "zc", len(ZHALF) - 1))
        o = T.zg[:, PW * p:PW * (p + n)]
        src = T.zw[:, 2048 * t:2048 * t + 4096].indirect(T.off[:, Q * t + 64 * p:Q * t + 64 * (p + n)])
        fn = {"a": lambda: S.activation(o, src, ACT.Copy), "v": lambda: V.tensor_copy(o, src)}[e]
        op(e, fn, zwin_keys[t] + [("off", t)], [("zg", i) for i in range(p, p + n)])
        done.update((t, "zg", i) for i in range(p, p + n))

    zbank = [("c", 0), "r5"]

    def zout(a, n):
        return T.pr2[:, 256 + a:256 + a + n] if a >= 256 else T.pc0[:, a:a + n]

    def zmax(t, c):
        need((t, "zg", 2 * c), (t, "zg", 2 * c + 1))
        if c < 2:
            need((t, "fin", 0))
        elif holder.get(5) != "z":
            assert (t, "zmax", 5 - c) not in done
            take("z", 5)
        o = CW * (c % 2)
        op("v", lambda: V.tensor_tensor_scan(T.zs[:, o:o + CW], T.zmask[:], T.zg[:, CW * c:CW * c + CW], 0.0, ALU.mult, ALU.max),
           ["zmask", ("zg", 2 * c), ("zg", 2 * c + 1)], [("zs", c % 2)])
        mms([(zout(CQ * c, CQ), T.mbm[:], T.zs[:, o + 15:o + CW:16], True, True)], [("zs", c % 2), "mats"], [], [zbank[c // 2]])

    def za(t, h):
        a, b = ZHALF[h]
        need(*[(t, "zmax", c) for c in range(a // CQ, b // CQ)])
        op("v", lambda: V.tensor_copy(T.zi[:, a:b], zout(a, b - a)), (), [("zi", h)], [zbank[h]])
        if h:
            holder[5] = None

    def zb(t, h):
        a, b = ZHALF[h]
        need((t, "za", h))
        op("v", lambda: V.tensor_scalar(T.zi[:, a:b], T.zi[:, a:b], 2, 15, ALU.arith_shift_right, ALU.bitwise_and), [("zi", h)], [("zi", h)])

    def zc(t, h):
        a, b = ZHALF[h]
        need((t, "zb", h))
        if h:
            need((t, "zc", h - 1))
        if t < 2:
            o = 2048 * (t + 2) + own
            op("v", lambda: V.tensor_copy(T.zw[:, o + a:o + b], T.zi[:, a:b]), [("zi", h)], [("zpart", h)])
            send("z%dc%d" % (t + 1, h), [("zpart", h)])
            if b == Q:
                wr["zq%d" % (t + 2)] = [("cv", count["cv"])]
                if t == 1:
                    op("g", lambda: g.affine_select(T.yzs[:, 1:1024:2], zq(3), [[0, Q]], ALU.is_ge, 0.0, 0, 0), ["zq3"], ["yzodd"])
        else:
            op("v", lambda: V.tensor_copy(T.yzs[:, 2 * a:2 * b:2], T.zi[:, a:b]), [("zi", h)], [("zpart", h)])
            deps("s", [("zpart", h), "yzodd"], (), ())
            g.sync.dma_start(T.yz[:, 2 * a:2 * b], T.yzs[:, 2 * a:2 * b]).then_inc(T.sem.outs, 16)
            outs[0] += 16

    def aside(t, i):
        if t == 0:
            deps("g", ["vO0", "vin0"], (), ())
            g.dma_start(T.w1[:, 0:2048], T.w0[:, 2048:4096]).then_inc(T.sem.cast, 16)
            wr["cast"] = [("cast", 16)]
        if t == 2:
            o = 4096 + own
            op("g", lambda: g.affine_select(T.yvs[:, 1:1024:2], T.w1[:, o:o + Q], [[0, Q]], ALU.is_ge, 0.0, 0, 0), vnew[1], ["yvodd"])

    def lst(t, i):
        if t == 0 and i == 0:
            list4(1)
        if t == 1 and i:
            need((0, "zc", len(ZHALF) - 1))
            if i > 1:
                need((t, "list", i - 1))
            (list1, list2, list3, list4)[i - 1](2)

    steps = {"dg": dg, "DG": lambda t, p: dg(t, p, 2), "ab": ab, "AB": lambda t, p: ab(t, p, 2), "sm": sm, "relu": relu, "diff": diff,
             "expw": expw, "sumw": sumw, "expr": expr, "high": high, "low": low, "bc": bc, "scan": scan,
             "SCAN": lambda t, p: scan(t, 2 * p, 2), "abm": abm, "self": self_, "scale": scale, "fin": fin, "zg": zg,
             "ZG": lambda t, c: zg(t, 2 * c, 2), "zv": lambda t, p: zg(t, p, 1, "v"), "zmax": zmax, "za": za, "zb": zb, "zc": zc,
             "aside": aside, "list": lst, "rep": lambda t, i: reps("g", 2, t + 1)}
    for t in range(4):
        for word in ORDER.split():
            late = word.startswith("-")
            name = word.strip("-0123456789")
            tt, i = t - late, int(word[late + len(name):])
            if 0 <= tt < 3:
                steps[name](tt, i)
                done.add((tt, name, i))

    g.wait_ge(T.sem.sent, sent[0])
    wait("s", [(s, v) for s, v in count.items()])
    g.sync.wait_ge(T.sem.outs, outs[0])
